import numpy as np, ml_dtypes
CORES = [9,25,41,57]
N = 4
BF = ml_dtypes.bfloat16
L, S, Q = 256, 5, 1280
def packed(rng, st):
    fr = np.diff(np.append(st, 2048)); sy = rng.permutation(256)[:len(st)]
    return np.stack([np.repeat(2048 * (fr - 1) + st, fr), np.repeat(sy, fr)])
def model(rng, n):
    return packed(rng, np.concatenate([[0], np.sort(rng.integers(0, 2048 - 8 * n + 1, n - 1)) + 8 * np.arange(1, n)]).astype(np.int64))
def both(m):
    return {"models": np.ascontiguousarray(m[:, :, 0]).astype(np.int32), "letters": np.ascontiguousarray(m[:, :, 1]).astype(np.int32)}
def models_of(rng, n):
    return both(np.stack([np.stack([model(rng, int(n[r, g])) for g in range(8)]) for r in range(N)]))
def some_states(rng):
    return np.clip(np.exp2(12 + 8 * rng.random((N, 8, L))), 4096, 1048575).astype(np.int32)
def some_bytes(rng):
    return rng.integers(0, 256, (N, 8, Q)).astype(np.int32)
def same(p):
    return np.repeat(p[None], N, axis=0).astype(np.int32)
def some_places(rng):
    return same(np.stack([rng.permutation(N * Q) for g in range(8)]))
def setup_inputs(rng):
    n = np.exp2(1 + 6.5 * rng.random((N, 8))).astype(np.int64); n[:, rng.integers(0, 8)] = 256
    m = models_of(rng, n)
    return {"states": some_states(rng), "models": m["models"], "letters": m["letters"], "stock": some_bytes(rng), "places": some_places(rng)}
def setup_inputs_every(rng):
    x = some_states(rng); x[:, :, 0] = 4096; x[:, :, L - 1] = 1048575
    m = models_of(rng, np.full((N, 8), 256)); p = some_places(rng); g = rng.permutation(8)
    p[:, g[0]] = np.arange(N * Q); p[:, g[1]] = np.arange(N * Q)[::-1]
    return {"states": x, "models": m["models"], "letters": m["letters"], "stock": some_bytes(rng), "places": p}
def setup_inputs_dry(rng):
    d = setup_inputs(rng); n = np.exp2(1 + 6.5 * rng.random((N, 8))).astype(np.int64); g = rng.permutation(8); p = rng.permutation(N)
    n[:, g[:3]] = 1
    for i in range(5):
        n[p[i % N], g[3 + i]] = 1
    d.update(models_of(rng, n)); return d
def setup_inputs_edge(rng):
    k = 2 ** rng.integers(4, 11, (N, 8, 1)); up = 4096 // k; a = rng.integers(0, 2048, (N, 8, L)) // k * k
    kind = rng.integers(0, 4, (N, 8, L)); kind[:, :, :4] = np.arange(4)
    x = np.where(kind == 0, 2048 * up + a, np.where(kind == 1, 2048 * (up - 1) + a + k - 1, np.where(kind == 2, 4096, 1048575)))
    m = both(np.stack([np.stack([packed(rng, np.arange(0, 2048, int(k[r, g, 0]))) for g in range(8)]) for r in range(N)]))
    return {"states": x.astype(np.int32), "models": m["models"], "letters": m["letters"], "stock": (255 * rng.integers(0, 2, (N, 8, Q))).astype(np.int32), "places": some_places(rng)}
def setup_inputs_few(rng):
    x = rng.integers(2 ** 19, 2 ** 20, (N, 8, L)); x[:, :, 0] = rng.integers(4096, 8192, (N, 8)); x[:, :, L - 1] = rng.integers(4096, 8192, (N, 8)); x[:, :, 1] = rng.integers(8192, 16384, (N, 8))
    p = rng.permutation(N); m = both(np.stack([np.stack([packed(rng, np.arange(0, 2048, 8 if p[g % N] == r else 1024)) for g in range(8)]) for r in range(N)]))
    return {"states": x.astype(np.int32), "models": m["models"], "letters": m["letters"], "stock": some_bytes(rng), "places": some_places(rng)}
def setup_inputs_spread(rng):
    slot = np.arange(2048); e = np.floor((slot + 1) * rng.random((N, 8, 2048)) ** 3).astype(np.int64); e = np.minimum(e, slot)
    lo = np.maximum(e, 7); w = np.minimum(lo + np.floor((2048 - lo) * rng.random((N, 8, 2048)) ** 4).astype(np.int64), 2047)
    m = 2048 * w + slot - e
    b = np.minimum(np.floor(256 * rng.random((N, 8, Q)) ** 6), 255)
    return {"states": some_states(rng), "models": m.astype(np.int32), "letters": rng.integers(0, 256, (N, 8, 2048)).astype(np.int32), "stock": b.astype(np.int32), "places": some_places(rng)}
def check_inputs(d):
    x, t, a, b, p = d["states"], d["models"].astype(np.int64), d["letters"], d["stock"], d["places"]; bad = []; slot = np.arange(2048)
    if not ((x >= 4096) & (x < 1048576)).all(): bad.append("states")
    if not ((t >= 14336) & (t < 4194304) & ((t & 2047) <= slot) & (slot <= (t & 2047) + (t >> 11))).all(): bad.append("models")
    if not ((a >= 0) & (a < 256)).all(): bad.append("letters")
    if not ((b >= 0) & (b < 256)).all(): bad.append("stock")
    if not ((np.sort(p, axis=2) == np.arange(N * Q)).all() and (p == p[:1]).all()): bad.append("places")
    return bad
def whole(b):
    return np.ascontiguousarray(b.transpose(1, 2, 0)).reshape(8, -1)
def line(v, s):
    return np.ascontiguousarray(np.roll(v, -s, axis=0).transpose(1, 0, 2)).reshape(8, -1)
def unline(u, s):
    return np.roll(u.reshape(8, N, L).transpose(1, 0, 2), s, axis=0)
def reference(states, models, letters, stock, places):
    x = states.astype(np.int64); t = models.astype(np.int64); pool = whole(stock.astype(np.int64)); seq = places[0].astype(np.int64)
    syms = np.zeros((N, 8, S * L), np.int32); used = np.zeros(8, np.int64)
    for s in range(S):
        slot = x & 2047; e = np.take_along_axis(t, slot, 2)
        syms[:, :, s * L:(s + 1) * L] = np.take_along_axis(letters, slot, 2)
        x = ((e >> 11) + 1) * (x >> 11) + slot - (e & 2047)
        reads = x < 4096; w = line(reads, s).astype(np.int64)
        at = used[:, None] + np.add.accumulate(w, axis=1) - w
        x = np.where(reads, 256 * x + unline(np.take_along_axis(pool, np.take_along_axis(seq, at, 1), 1), s), x)
        used = used + np.add.reduce(w, axis=1)
    return {"syms": np.asarray(syms, np.float32), "last": np.asarray(x, np.float32)}

@@ -1,0 +1,292 @@
+import numpy as np
+from concourse.bass import DstId, RemoteDMATransfer
+from concourse.mybir import dt, AluOpType, ActivationFunctionType
+
+SCRATCH = {
+    "stgm": ("dram", [4, 128, 64], "int32"), "landm": ("dram", [4, 128, 64], "int32"),
+    "stgs": ("dram", [4, 128, 32], "float32"), "lands": ("dram", [4, 128, 32], "float32"),
+    "back1": ("dram", [4, 128, 64], "float32"), "back2": ("dram", [4, 128, 32], "float32"),
+    "win": ("sbuf", [128, 4096], "int32"), "pool": ("sbuf", [128, 5120], "float32"), "bt": ("sbuf", [128, 5136], "bfloat16"),
+    "zero": ("sbuf", [128, 512], "float32"), "padz": ("sbuf", [128, 32], "float32"),
+    "pl": ("sbuf", [128, 10, 16], "int32"), "pa": ("sbuf", [128, 10, 16], "int32"), "pb": ("sbuf", [128, 10, 16], "int32"),
+    "pc": ("sbuf", [128, 10, 16], "float32"), "pi3": ("sbuf", [128, 10, 32], "float32"),
+    "pt": ("sbuf", [128, 320], "float32"), "order": ("sbuf", [128, 320], "uint16"),
+    "dm": ("sbuf", [128, 128], "float32"), "rowkey": ("sbuf", [128, 256], "float32"),
+    "coli": ("sbuf", [128, 8], "int32"), "colj": ("sbuf", [128, 8], "int32"), "colk": ("sbuf", [128, 8], "float32"),
+    "flags": ("sbuf", [128, 4], "float32"), "sw": ("sbuf", [128, 512], "float32"), "swb": ("sbuf", [128, 512], "bfloat16"),
+    "tri": ("sbuf", [128, 512], "bfloat16"), "allm": ("sbuf", [128, 128], "bfloat16"), "ones": ("sbuf", [128, 16], "bfloat16"),
+    "x0": ("sbuf", [128, 16], "float32"), "x0k": ("sbuf", [128, 16], "float32"),
+    "xi": ("sbuf", [128, 80], "int32"), "xf": ("sbuf", [128, 80], "float32"), "slot": ("sbuf", [128, 80], "int32"),
+    "lst": ("sbuf", [128, 80], "uint16"), "ra": ("sbuf", [128, 1280], "float32"), "ta": ("sbuf", [128, 1280], "float32"),
+    "gg": ("sbuf", [128, 80], "int32"), "yh": ("sbuf", [128, 80], "int32"), "q2": ("sbuf", [128, 80], "float32"),
+    "t2": ("sbuf", [128, 80], "float32"), "xn": ("sbuf", [128, 80], "float32"), "wr": ("sbuf", [128, 80], "bfloat16"),
+    "cs": ("sbuf", [128, 80], "bfloat16"), "mm": ("sbuf", [128, 80], "float32"), "xw": ("sbuf", [128, 80], "float32"),
+    "uu": ("sbuf", [128, 80], "float32"), "vv": ("sbuf", [128, 80], "float32"), "idx": ("sbuf", [128, 80], "uint16"),
+    "rb": ("sbuf", [128, 1280], "bfloat16"), "tb": ("sbuf", [128, 1280], "bfloat16"),
+    "res1": ("sbuf", [128, 64], "float32"), "res2": ("sbuf", [128, 32], "float32"),
+    "psa0": ("psum", [128, 512], "float32"), "psa1": ("psum", [128, 512], "float32"),
+    "psb0": ("psum", [128, 512], "float32"), "psb1": ("psum", [128, 512], "float32"),
+    "psc0": ("psum", [128, 512], "float32"), "psc1": ("psum", [128, 512], "float32"),
+}
+SEMAPHORES = ["v", "a", "t", "k", "dstage", "dpad", "down", "down2", "dpl", "gcast", "dwin", "dx", "dpool", "rs", "rm", "r1",
+              "r2", "loc", "dback1", "dback2", "dout", "dout2"]
+
+
+def rank_program(g, core, T, topo):
+    rank = T.rank_of(core)
+    if rank is None:
+        return
+    A = AluOpType
+    COPY = ActivationFunctionType.Copy
+    S, L = 5, 256
+    others = [c for c in T.cores if c != core]
+    K = 2047 * 2048
+
+    queues = {"g": g, "v": g.vector, "a": g.scalar, "t": g.tensor, "y": g.sync}
+    count = {"v": 0, "a": 0, "t": 0, "k": 0}
+    seen = {}
+
+    def need(q, *tokens):
+        for name, n in tokens:
+            if n > seen.get((q, name), 0):
+                queues[q].wait_ge(T.sem[name], n)
+                seen[(q, name)] = n
+
+    def done(name, call):
+        call.then_inc(T.sem[name], 1)
+        count[name] += 1
+        return (name, count[name])
+
+    def v(call):
+        return done("v", call)
+
+    def ts(out, in0, s1, s2, op0, op1=None):
+        if op1 is None:
+            return v(g.vector.tensor_scalar(out, in0, s1, s2, op0))
+        return v(g.vector.tensor_scalar(out, in0, s1, s2, op0, op1))
+
+    def tt(out, a, b, op):
+        return v(g.vector.tensor_tensor(out, a, b, op))
+
+    def dst(c):
+        rid, pid, _ = topo.addr(c)
+        return DstId(rid=rid, pnc=pid)
+
+    def bits(engines):
+        m = 0
+        for e in engines:
+            m |= 1 << e
+        return m
+
+    def spread(src, land, sem):
+        out = []
+        for i, c in enumerate(others):
+            es = topo.engines(core, c)
+            out.append(RemoteDMATransfer(src=src[T.rank_of(c)], dst=land[rank], dst_ids=[dst(c)],
+                                         dma_engine_mask=bits(es[2 * i:2 * i + 2]), remote_sem=T.sem[sem]))
+        g.remote_dma_fused(out, local_sem=T.sem.loc)
+
+    def same(src, land, sem):
+        es = topo.engines(core, others[0])
+        g.remote_dma_fused([RemoteDMATransfer(srcs=[src], dsts=[land[rank] for c in others], dst_ids=[dst(c) for c in others],
+                                              dma_engine_mask=bits(es), remote_sem=T.sem[sem])], local_sem=T.sem.loc)
+
+    g.dma_start(T.stgs[:, 0:80, :], T.stock[:]).then_inc(T.sem.gcast, 16)
+    g.dma_start(T.stgs[:, 80:96, :], T.states[:]).then_inc(T.sem.gcast, 16)
+    g.sync.dma_start(T.stgm[:, 0:64, :], T.models[:]).then_inc(T.sem.dstage, 16)
+    g.sync.dma_start(T.stgm[:, 64:128, :], T.letters[:]).then_inc(T.sem.dstage, 16)
+    g.sync.dma_start(T.landm[rank, 0:64, :], T.models[2 * rank:2 * rank + 2, :]).then_inc(T.sem.down, 16)
+    g.sync.dma_start(T.landm[rank, 64:128, :], T.letters[2 * rank:2 * rank + 2, :]).then_inc(T.sem.down, 16)
+    vpad = v(g.vector.memset(T.padz[:], 0.0))
+    need("a", vpad)
+    g.scalar.dma_start(T.stgs[:, 96:128, :], T.padz[:]).then_inc(T.sem.dpad, 16)
+    for a in range(4):
+        g.scalar.dma_start(T.pl[32 * a:32 * a + 32, :, :], T.places[2 * rank + a // 2, :]).then_inc(T.sem.dpl, 16)
+    dpl = ("dpl", 64)
+
+    k1 = done("k", g.iota(T.coli[:, 0:4], [[-16, 4]], 64, 1))
+    k1 = done("k", g.iota(T.coli[:, 4:8], [[0, 4]], 0, 1))
+    k1 = done("k", g.iota(T.dm[:], [[1, 128]], 0, -1, allow_small_or_imprecise_dtypes=True))
+    k2 = done("k", g.iota(T.rowkey[:], [[0, 4], [1, 64]], 0, 0, allow_small_or_imprecise_dtypes=True))
+
+    need("g", ("gcast", 32), ("dpad", 16))
+    spread(T.stgs, T.lands, "rs")
+    need("g", ("dstage", 32))
+    spread(T.stgm, T.landm, "rm")
+
+    vz = v(g.vector.memset(T.zero[:], 0.0))
+    vwin = v(g.vector.memset(T.win[:], 0))
+    v(g.vector.memset(T.bt[:, 0:1], 0.0))
+    v(g.vector.memset(T.ones[:], 1.0))
+    need("v", dpl)
+    p1 = ts(T.pa[:], T.pl[:], 3, None, A.bitwise_and)
+    p2 = ts(T.pb[:], T.pl[:], 2, None, A.arith_shift_right)
+    need("v", p1)
+    p3 = ts(T.pc[:], T.pa[:], 1280.0, None, A.mult)
+    need("v", k1)
+    ts(T.colj[:, 0:4], T.coli[:, 0:4], 63, None, A.bitwise_and)
+    c2 = ts(T.colj[:, 4:8], T.coli[:, 4:8], 16, None, A.bitwise_and)
+    need("v", p3)
+    tt(T.pi3[:, :, 0:16], T.pb[:], T.pc[:], A.add)
+    p4 = tt(T.pi3[:, :, 16:32], T.pb[:], T.pc[:], A.add)
+    need("v", c2)
+    ts(T.flags[:, 0:1], T.colj[:, 4:5], 0.0, None, A.is_equal)
+    ts(T.flags[:, 1:2], T.colj[:, 4:5], 16.0, None, A.is_equal)
+    ts(T.flags[:, 2:3], T.coli[:, 4:5], 64.0, None, A.is_lt)
+    ts(T.flags[:, 3:4], T.coli[:, 4:5], 64.0, None, A.is_ge)
+    c3 = v(g.vector.tensor_copy(T.colk[:, 0:4], T.colj[:, 0:4]))
+    need("v", p4)
+    for b in range(10):
+        p5 = v(g.vector.transpose(T.pt[:, 32 * b:32 * b + 32], T.pi3[:, b, :]))
+    need("v", p5)
+    for b in range(10):
+        vorder = v(g.vector.tensor_copy(T.order[:, b:320:10], T.pt[:, 32 * b:32 * b + 32]))
+    need("v", k2, c3)
+    for i, (d, f) in enumerate(((0.0, 0), (16.0, 0), (-16.0, 1), (0.0, 1))):
+        vsw = ts(T.sw[:, 128 * i:128 * i + 128], T.dm[:], d, T.flags[:, f:f + 1], A.is_equal, A.mult)
+
+    need("a", vz)
+    for i in range(10):
+        apool = done("a", g.scalar.activation(T.pool[:, 512 * i:512 * i + 512], T.zero[:], COPY))
+    need("y", ("gcast", 32))
+    g.sync.dma_start(T.lands[rank, 0:96, :], T.stgs[rank, 0:96, :]).then_inc(T.sem.down2, 16)
+    need("a", ("down2", 16), ("rs", 6))
+    for sg in range(2):
+        g.scalar.dma_start(T.x0[64 * sg:64 * sg + 64, :], T.lands[:, 80 + 8 * sg:88 + 8 * sg, :]).then_inc(T.sem.dx, 16)
+    need("a", apool)
+    for i in range(8):
+        sg = i // 4
+        g.scalar.dma_start(T.pool[16 * i:16 * i + 1, :], T.lands[:, 40 * sg:40 * sg + 40, :]).then_inc(T.sem.dpool, 16)
+    need("y", ("down", 32), ("rm", 6), vwin)
+    for kind in range(2):
+        for ga in range(2):
+            for sg in range(2):
+                p = 64 * sg + 16 * ga + kind
+                g.sync.dma_start(T.win[p:p + 33:32, :], T.landm[:, 64 * kind + 32 * sg:64 * kind + 32 * sg + 32, :]).then_inc(T.sem.dwin, 16)
+
+    def swap(ps, even, odd, mats):
+        t = g.tensor
+        t.matmul(ps[:, 0:16:2], mats[:, 0:128], even, True, False)
+        t.matmul(ps[:, 0:16:2], mats[:, 128:256], odd, False, True)
+        t.matmul(ps[:, 1:16:2], mats[:, 256:384], even, True, False)
+        return done("t", t.matmul(ps[:, 1:16:2], mats[:, 384:512], odd, False, True))
+
+    def chunk(s):
+        return done("a", g.scalar.activation(T.bt[:, 1 + 1024 * s:1025 + 1024 * s], T.pool[:].indirect(T.order[:, 64 * s:64 * s + 64]), COPY))
+
+    need("t", vsw, ("dx", 32))
+    tx = swap(T.psb1, T.x0[:, 0:16:2], T.x0[:, 1:16:2], T.sw)
+    need("v", ("dx", 32))
+    vx0k = ts(T.x0k[:], T.x0[:], float(K), None, A.add)
+    need("v", tx)
+    vxi = v(g.vector.tensor_copy(T.xi[:, 0:16], T.psb1[:, 0:16]))
+
+    need("a", ("dpool", 128), vorder)
+    chunks = [chunk(0), chunk(1)]
+    vtri = None
+    for s in range(S):
+        c = slice(16 * s, 16 * s + 16)
+        ev = slice(16 * s, 16 * s + 16, 2)
+        od = slice(16 * s + 1, 16 * s + 16, 2)
+        wide = slice(256 * s, 256 * s + 256)
+        psa, psb, psc = T["psa%d" % (s % 2)], T["psb%d" % (s % 2)], T["psc%d" % (s % 2)]
+        need("v", vxi)
+        vslot = ts(T.slot[:, c], T.xi[:, c], 2047, None, A.bitwise_and)
+        if s:
+            vxf = ts(T.xf[:, c], T.xi[:, c], float(K), None, A.add)
+            need("t", vxf)
+            tsa = swap(psa, T.xf[:, ev], T.xf[:, od], T.sw)
+            for q in range(s):
+                g.tensor.matmul(psc[:, 0:1], T.allm[:], T.cs[:, 16 * q + 15:16 * q + 16], q == 0, False)
+        need("v", vslot)
+        ts(T.lst[:, ev], T.slot[:, ev], 0.0, None, A.add)
+        vl = ts(T.lst[:, od], T.slot[:, od], 2048.0, None, A.add)
+        if s == 0:
+            for r in range(4):
+                for b in range(2):
+                    o = 64 - 16 * r + 64 * b
+                    ts(T.tri[:, 128 * r + 64 * b:128 * r + 64 * b + 64], T.rowkey[:, o:o + 64], T.colk[:, r:r + 1], T.flags[:, 2 + b:3 + b], A.is_gt, A.mult)
+            for b in range(2):
+                vtri = ts(T.allm[:, 64 * b:64 * b + 64], T.rowkey[:, 0:64], 0.0, T.flags[:, 2 + b:3 + b], A.mult, A.add)
+        need("v", vl, ("dwin", 128))
+        vr = v(g.vector.tensor_copy(T.ra[:, wide], T.win[:].indirect(T.lst[:, c])))
+        need("v", vr)
+        vt = v(g.vector.transpose(T.ta[:, wide], T.ra[:, wide]))
+        e = T.ta[:, 256 * s:256 * s + 256:16]
+        if s:
+            need("v", tsa)
+            xs = psa[:, 0:16]
+        else:
+            need("v", vx0k)
+            xs = T.x0k[:]
+        ts(T.yh[:, c], xs, 1.0 / 2048, 0.500244140625, A.mult, A.add)
+        need("v", vt)
+        vg = ts(T.gg[:, c], e, 1.0 / 2048, -2047.499755859375, A.mult, A.add)
+        vq = tt(T.q2[:, c], xs, e, A.subtract)
+        need("v", vg)
+        vt2 = tt(T.t2[:, c], T.gg[:, c], T.yh[:, c], A.mult)
+        need("v", vt2)
+        vxn = tt(T.xn[:, c], T.t2[:, c], T.q2[:, c], A.add)
+        need("v", vxn)
+        vw = ts(T.wr[:, c], T.xn[:, c], 4096.0, None, A.is_lt)
+        need("v", vw)
+        vcs = v(g.vector.tensor_tensor_scan(T.cs[:, c], T.ones[:], T.wr[:, c], 0.0, A.mult, A.add))
+        need("t", vcs, vtri)
+        r = s % 4
+        tb = done("t", g.tensor.matmul(psc[:, 0:1], T.tri[:, 128 * r:128 * r + 128], T.cs[:, 16 * s + 15:16 * s + 16], s == 0, True))
+        vm = ts(T.mm[:, c], T.wr[:, c], 255.0, 1.0, A.mult, A.add)
+        vu = ts(T.uu[:, c], T.wr[:, c], 8192.0, -8192.0, A.mult, A.add)
+        need("v", vm)
+        vxw = tt(T.xw[:, c], T.mm[:, c], T.xn[:, c], A.mult)
+        if s < S - 1:
+            need("t", vxw)
+            tw = swap(psb, T.xw[:, ev], T.xw[:, od], T.sw)
+        need("v", vu, vcs)
+        vv = tt(T.vv[:, c], T.uu[:, c], T.cs[:, c], A.add)
+        need("v", vv, tb)
+        vi = ts(T.idx[:, c], T.vv[:, c], psc[:, 0:1], None, A.add)
+        need("v", vi, chunks[s])
+        vrb = v(g.vector.tensor_copy(T.rb[:, wide], T.bt[:, 0:1025 + 1024 * s].indirect(T.idx[:, c])))
+        need("v", vrb)
+        vtb = v(g.vector.transpose(T.tb[:, wide], T.rb[:, wide]))
+        byte = T.tb[:, 256 * s:256 * s + 256:16]
+        need("a", vt)
+        sy = T.res1[:, c] if s < S - 1 else T.res2[:, 16:32]
+        asy = done("a", g.scalar.activation(sy, T.ta[:, 256 * s + 1:256 * s + 256:16], COPY))
+        if s + 2 < S:
+            chunks.append(chunk(s + 2))
+        if s == 2:
+            need("a", vsw)
+            aswb = done("a", g.scalar.activation(T.swb[:], T.sw[:], COPY))
+        if s == S - 2:
+            need("g", asy)
+            same(T.res1[:], T.back1, "r1")
+            need("y", asy)
+            g.sync.dma_start(T.back1[rank], T.res1[:]).then_inc(T.sem.dback1, 16)
+        if s < S - 1:
+            need("v", vtb, tw)
+            vxi = tt(T.xi[:, 16 * s + 16:16 * s + 32], psb[:, 0:16], byte, A.add)
+        else:
+            need("t", vtb, aswb)
+            tl = swap(psb, T.tb[:, 256 * s:256 * s + 256:32], T.tb[:, 256 * s + 16:256 * s + 256:32], T.swb)
+            need("v", tl)
+            vlast = tt(T.res2[:, 0:16], psb[:, 0:16], T.xw[:, c], A.add)
+
+    need("g", vlast, asy)
+    same(T.res2[:], T.back2, "r2")
+    need("y", ("r1", 24), ("dback1", 16))
+    mine = [slice(64 * sg + 16 * rank, 64 * sg + 16 * rank + 16) for sg in range(2)]
+    need("a", vlast, asy)
+    g.scalar.dma_start(T.back2[rank], T.res2[:]).then_inc(T.sem.dback2, 16)
+    for s in range(S - 1):
+        for sg in range(2):
+            g.sync.dma_start(T.syms[sg:8:2, L * s:L * s + L], T.back1[:, mine[sg], 16 * s:16 * s + 16]).then_inc(T.sem.dout, 16)
+    need("y", ("r2", 24), ("dback2", 16))
+    for sg in range(2):
+        g.sync.dma_start(T.last[sg:8:2, :], T.back2[:, mine[sg], 0:16]).then_inc(T.sem.dout, 16)
+    need("a", ("r2", 24), ("dback2", 16))
+    for sg in range(2):
+        g.scalar.dma_start(T.syms[sg:8:2, L * (S - 1):L * S], T.back2[:, mine[sg], 16:32]).then_inc(T.sem.dout2, 16)
+    need("y", ("dout", 160))
+    need("a", ("dout2", 32))
+    need("g", ("loc", 28), ("v", count["v"]), ("a", count["a"]), ("t", count["t"]), ("k", count["k"]))

@@ -7,20 +7,24 @@ SCRATCH = {
     "stgs": ("dram", [4, 128, 32], "float32"), "lands": ("dram", [4, 128, 32], "float32"),
     "back1": ("dram", [4, 128, 64], "float32"), "back2": ("dram", [4, 128, 32], "float32"),
     "win": ("sbuf", [128, 4096], "int32"), "pool": ("sbuf", [128, 5120], "float32"), "bt": ("sbuf", [128, 5136], "bfloat16"),
-    "zero": ("sbuf", [128, 512], "float32"), "padz": ("sbuf", [128, 32], "float32"),
+    "zero": ("sbuf", [128, 512], "bfloat16"), "padz": ("sbuf", [128, 32], "float32"),
     "pl": ("sbuf", [128, 10, 16], "int32"), "pa": ("sbuf", [128, 10, 16], "int32"), "pb": ("sbuf", [128, 10, 16], "int32"),
     "pc": ("sbuf", [128, 10, 16], "float32"), "pi3": ("sbuf", [128, 10, 32], "float32"),
     "pt": ("sbuf", [128, 320], "float32"), "order": ("sbuf", [128, 320], "uint16"),
     "dm": ("sbuf", [128, 128], "float32"), "rowkey": ("sbuf", [128, 256], "float32"),
     "coli": ("sbuf", [128, 8], "int32"), "colj": ("sbuf", [128, 8], "int32"), "colk": ("sbuf", [128, 8], "float32"),
-    "flags": ("sbuf", [128, 4], "float32"), "sw": ("sbuf", [128, 512], "float32"), "swb": ("sbuf", [128, 512], "bfloat16"),
+    "flags": ("sbuf", [128, 4], "float32"), "swh": ("sbuf", [128, 512], "float16"), "swb": ("sbuf", [128, 512], "bfloat16"),
+    "c16": ("sbuf", [128, 128], "bfloat16"),
     "tri": ("sbuf", [128, 512], "bfloat16"), "allm": ("sbuf", [128, 128], "bfloat16"), "ones": ("sbuf", [128, 16], "bfloat16"),
-    "x0": ("sbuf", [128, 16], "float32"), "x0k": ("sbuf", [128, 16], "float32"),
-    "xi": ("sbuf", [128, 80], "int32"), "xf": ("sbuf", [128, 80], "float32"), "slot": ("sbuf", [128, 80], "int32"),
+    "x0": ("sbuf", [128, 16], "float32"), "x0i": ("sbuf", [128, 16], "int32"), "sl0": ("sbuf", [128, 16], "int32"),
+    "sh0": ("sbuf", [128, 16], "float16"),
+    "xf": ("sbuf", [128, 80], "float32"), "slf": ("sbuf", [128, 80], "float32"),
     "lst": ("sbuf", [128, 80], "uint16"), "ra": ("sbuf", [128, 1280], "float32"), "ta": ("sbuf", [128, 1280], "float32"),
     "gg": ("sbuf", [128, 80], "int32"), "yh": ("sbuf", [128, 80], "int32"), "q2": ("sbuf", [128, 80], "float32"),
+    "rr": ("sbuf", [128, 80], "float32"),
     "t2": ("sbuf", [128, 80], "float32"), "xn": ("sbuf", [128, 80], "float32"), "wr": ("sbuf", [128, 80], "bfloat16"),
-    "cs": ("sbuf", [128, 80], "bfloat16"), "mm": ("sbuf", [128, 80], "float32"), "xw": ("sbuf", [128, 80], "float32"),
+    "cs": ("sbuf", [128, 80], "bfloat16"), "mm": ("sbuf", [128, 80], "float32"), "xwi": ("sbuf", [128, 80], "int32"),
+    "xwk": ("sbuf", [128, 80], "float32"), "sl": ("sbuf", [128, 80], "int32"), "sh": ("sbuf", [128, 80], "float16"),
     "uu": ("sbuf", [128, 80], "float32"), "vv": ("sbuf", [128, 80], "float32"), "idx": ("sbuf", [128, 80], "uint16"),
     "rb": ("sbuf", [128, 1280], "bfloat16"), "tb": ("sbuf", [128, 1280], "bfloat16"),
     "res1": ("sbuf", [128, 64], "float32"), "res2": ("sbuf", [128, 32], "float32"),
@@ -41,6 +45,7 @@ def rank_program(g, core, T, topo):
     S, L = 5, 256
     others = [c for c in T.cores if c != core]
     K = 2047 * 2048
+    FILL = 3328
 
     queues = {"g": g, "v": g.vector, "a": g.scalar, "t": g.tensor, "y": g.sync}
     count = {"v": 0, "a": 0, "t": 0, "k": 0}
@@ -104,20 +109,22 @@ def rank_program(g, core, T, topo):
         g.scalar.dma_start(T.pl[32 * a:32 * a + 32, :, :], T.places[2 * rank + a // 2, :]).then_inc(T.sem.dpl, 16)
     dpl = ("dpl", 64)
 
-    k1 = done("k", g.iota(T.coli[:, 0:4], [[-16, 4]], 64, 1))
+    kwin = done("k", g.iota(T.win[:, FILL:4096], [[0, 4096 - FILL]], 0, 0))
+    done("k", g.iota(T.coli[:, 0:4], [[-16, 4]], 64, 1))
     k1 = done("k", g.iota(T.coli[:, 4:8], [[0, 4]], 0, 1))
-    k1 = done("k", g.iota(T.dm[:], [[1, 128]], 0, -1, allow_small_or_imprecise_dtypes=True))
-    k2 = done("k", g.iota(T.rowkey[:], [[0, 4], [1, 64]], 0, 0, allow_small_or_imprecise_dtypes=True))
 
     need("g", ("gcast", 32), ("dpad", 16))
     spread(T.stgs, T.lands, "rs")
     need("g", ("dstage", 32))
     spread(T.stgm, T.landm, "rm")
+    k2 = done("k", g.iota(T.dm[:], [[1, 128]], 0, -1, allow_small_or_imprecise_dtypes=True))
+    k3 = done("k", g.iota(T.rowkey[:], [[0, 4], [1, 64]], 0, 0, allow_small_or_imprecise_dtypes=True))
 
     vz = v(g.vector.memset(T.zero[:], 0.0))
-    vwin = v(g.vector.memset(T.win[:], 0))
+    vwin = v(g.vector.memset(T.win[:, 0:FILL], 0))
     v(g.vector.memset(T.bt[:, 0:1], 0.0))
     v(g.vector.memset(T.ones[:], 1.0))
+    vc16 = v(g.vector.memset(T.c16[:], 16.0))
     need("v", dpl)
     p1 = ts(T.pa[:], T.pl[:], 3, None, A.bitwise_and)
     p2 = ts(T.pb[:], T.pl[:], 2, None, A.arith_shift_right)
@@ -143,7 +150,7 @@ def rank_program(g, core, T, topo):
         vorder = v(g.vector.tensor_copy(T.order[:, b:320:10], T.pt[:, 32 * b:32 * b + 32]))
     need("v", k2, c3)
     for i, (d, f) in enumerate(((0.0, 0), (16.0, 0), (-16.0, 1), (0.0, 1))):
-        vsw = ts(T.sw[:, 128 * i:128 * i + 128], T.dm[:], d, T.flags[:, f:f + 1], A.is_equal, A.mult)
+        vsw = ts(T.swh[:, 128 * i:128 * i + 128], T.dm[:], d, T.flags[:, f:f + 1], A.is_equal, A.mult)
 
     need("a", vz)
     for i in range(10):
@@ -157,120 +164,128 @@ def rank_program(g, core, T, topo):
     for i in range(8):
         sg = i // 4
         g.scalar.dma_start(T.pool[16 * i:16 * i + 1, :], T.lands[:, 40 * sg:40 * sg + 40, :]).then_inc(T.sem.dpool, 16)
-    need("y", ("down", 32), ("rm", 6), vwin)
+    need("y", ("down", 32), ("rm", 6), vwin, kwin)
     for kind in range(2):
         for ga in range(2):
             for sg in range(2):
                 p = 64 * sg + 16 * ga + kind
                 g.sync.dma_start(T.win[p:p + 33:32, :], T.landm[:, 64 * kind + 32 * sg:64 * kind + 32 * sg + 32, :]).then_inc(T.sem.dwin, 16)
 
-    def swap(ps, even, odd, mats):
-        t = g.tensor
-        t.matmul(ps[:, 0:16:2], mats[:, 0:128], even, True, False)
-        t.matmul(ps[:, 0:16:2], mats[:, 128:256], odd, False, True)
-        t.matmul(ps[:, 1:16:2], mats[:, 256:384], even, True, False)
-        return done("t", t.matmul(ps[:, 1:16:2], mats[:, 384:512], odd, False, True))
+    mm = g.tensor.matmul
+
+    def swap(ps, even, odd, mats, offset=None):
+        if offset is not None:
+            mm(ps[:, 1:16:2], T.c16[:], T.ones[:, 0:8], True, False)
+        if offset is not None:
+            need("t", offset)
+        mm(ps[:, 1:16:2], mats[:, 256:384], even, offset is None, False)
+        mm(ps[:, 1:16:2], mats[:, 384:512], odd, False, True)
+        mm(ps[:, 0:16:2], mats[:, 0:128], even, True, False)
+        return done("t", mm(ps[:, 0:16:2], mats[:, 128:256], odd, False, True))
 
     def chunk(s):
         return done("a", g.scalar.activation(T.bt[:, 1 + 1024 * s:1025 + 1024 * s], T.pool[:].indirect(T.order[:, 64 * s:64 * s + 64]), COPY))
 
-    need("t", vsw, ("dx", 32))
-    tx = swap(T.psb1, T.x0[:, 0:16:2], T.x0[:, 1:16:2], T.sw)
     need("v", ("dx", 32))
-    vx0k = ts(T.x0k[:], T.x0[:], float(K), None, A.add)
+    n1 = v(g.vector.tensor_copy(T.x0i[:], T.x0[:]))
+    vxs = ts(T.xf[:, 0:16], T.x0[:], float(K), None, A.add)
+    need("v", n1)
+    n2 = ts(T.sl0[:], T.x0i[:], 2047, None, A.bitwise_and)
+    need("v", n2)
+    n3 = v(g.vector.tensor_copy(T.sh0[:], T.sl0[:]))
+    need("t", vc16, vsw)
+    tx = swap(T.psb1, T.sh0[:, 0:16:2], T.sh0[:, 1:16:2], T.swh, n3)
+    need("v", k3)
+    for r in range(4):
+        for b in range(2):
+            o = 64 - 16 * r + 64 * b
+            ts(T.tri[:, 128 * r + 64 * b:128 * r + 64 * b + 64], T.rowkey[:, o:o + 64], T.colk[:, r:r + 1], T.flags[:, 2 + b:3 + b], A.is_gt, A.mult)
+    for b in range(2):
+        vtri = ts(T.allm[:, 64 * b:64 * b + 64], T.rowkey[:, 0:64], 0.0, T.flags[:, 2 + b:3 + b], A.mult, A.add)
+    need("v", vsw)
+    vswb = v(g.vector.tensor_copy(T.swb[:], T.swh[:]))
     need("v", tx)
-    vxi = v(g.vector.tensor_copy(T.xi[:, 0:16], T.psb1[:, 0:16]))
+    vl = v(g.vector.tensor_copy(T.lst[:, 0:16], T.psb1[:, 0:16]))
 
     need("a", ("dpool", 128), vorder)
     chunks = [chunk(0), chunk(1)]
-    vtri = None
     for s in range(S):
         c = slice(16 * s, 16 * s + 16)
         ev = slice(16 * s, 16 * s + 16, 2)
         od = slice(16 * s + 1, 16 * s + 16, 2)
+        nx = slice(16 * s + 16, 16 * s + 32)
         wide = slice(256 * s, 256 * s + 256)
         psa, psb, psc = T["psa%d" % (s % 2)], T["psb%d" % (s % 2)], T["psc%d" % (s % 2)]
-        need("v", vxi)
-        vslot = ts(T.slot[:, c], T.xi[:, c], 2047, None, A.bitwise_and)
-        if s:
-            vxf = ts(T.xf[:, c], T.xi[:, c], float(K), None, A.add)
-            need("t", vxf)
-            tsa = swap(psa, T.xf[:, ev], T.xf[:, od], T.sw)
-            for q in range(s):
-                g.tensor.matmul(psc[:, 0:1], T.allm[:], T.cs[:, 16 * q + 15:16 * q + 16], q == 0, False)
-        need("v", vslot)
-        ts(T.lst[:, ev], T.slot[:, ev], 0.0, None, A.add)
-        vl = ts(T.lst[:, od], T.slot[:, od], 2048.0, None, A.add)
-        if s == 0:
-            for r in range(4):
-                for b in range(2):
-                    o = 64 - 16 * r + 64 * b
-                    ts(T.tri[:, 128 * r + 64 * b:128 * r + 64 * b + 64], T.rowkey[:, o:o + 64], T.colk[:, r:r + 1], T.flags[:, 2 + b:3 + b], A.is_gt, A.mult)
-            for b in range(2):
-                vtri = ts(T.allm[:, 64 * b:64 * b + 64], T.rowkey[:, 0:64], 0.0, T.flags[:, 2 + b:3 + b], A.mult, A.add)
+        for q in range(s):
+            mm(psc[:, 0:1], T.allm[:], T.cs[:, 16 * q + 15:16 * q + 16], q == 0, False)
         need("v", vl, ("dwin", 128))
         vr = v(g.vector.tensor_copy(T.ra[:, wide], T.win[:].indirect(T.lst[:, c])))
+        if s:
+            need("v", tby)
+            vxs = tt(T.xf[:, c], T["psa%d" % ((s - 1) % 2)][:, 0:16], T.xwk[:, 16 * s - 16:16 * s], A.add)
+        xs = T.xf[:, c]
         need("v", vr)
         vt = v(g.vector.transpose(T.ta[:, wide], T.ra[:, wide]))
         e = T.ta[:, 256 * s:256 * s + 256:16]
-        if s:
-            need("v", tsa)
-            xs = psa[:, 0:16]
-        else:
-            need("v", vx0k)
-            xs = T.x0k[:]
+        need("v", vxs)
         ts(T.yh[:, c], xs, 1.0 / 2048, 0.500244140625, A.mult, A.add)
         need("v", vt)
         vg = ts(T.gg[:, c], e, 1.0 / 2048, -2047.499755859375, A.mult, A.add)
         vq = tt(T.q2[:, c], xs, e, A.subtract)
         need("v", vg)
         vt2 = tt(T.t2[:, c], T.gg[:, c], T.yh[:, c], A.mult)
-        need("v", vt2)
+        need("v", vq)
+        vrr = ts(T.rr[:, c], T.q2[:, c], -1.0, 4096.0, A.mult, A.add)
+        need("v", vt2, vrr)
+        vw = tt(T.wr[:, c], T.t2[:, c], T.rr[:, c], A.is_lt)
         vxn = tt(T.xn[:, c], T.t2[:, c], T.q2[:, c], A.add)
-        need("v", vxn)
-        vw = ts(T.wr[:, c], T.xn[:, c], 4096.0, None, A.is_lt)
         need("v", vw)
         vcs = v(g.vector.tensor_tensor_scan(T.cs[:, c], T.ones[:], T.wr[:, c], 0.0, A.mult, A.add))
         need("t", vcs, vtri)
         r = s % 4
-        tb = done("t", g.tensor.matmul(psc[:, 0:1], T.tri[:, 128 * r:128 * r + 128], T.cs[:, 16 * s + 15:16 * s + 16], s == 0, True))
+        tb = done("t", mm(psc[:, 0:1], T.tri[:, 128 * r:128 * r + 128], T.cs[:, 16 * s + 15:16 * s + 16], s == 0, True))
         vm = ts(T.mm[:, c], T.wr[:, c], 255.0, 1.0, A.mult, A.add)
         vu = ts(T.uu[:, c], T.wr[:, c], 8192.0, -8192.0, A.mult, A.add)
-        need("v", vm)
-        vxw = tt(T.xw[:, c], T.mm[:, c], T.xn[:, c], A.mult)
-        if s < S - 1:
-            need("t", vxw)
-            tw = swap(psb, T.xw[:, ev], T.xw[:, od], T.sw)
+        need("v", vm, vxn)
+        vxw = tt(T.xwi[:, c], T.mm[:, c], T.xn[:, c], A.mult)
         need("v", vu, vcs)
         vv = tt(T.vv[:, c], T.uu[:, c], T.cs[:, c], A.add)
+        if s < S - 1:
+            need("v", vxw)
+            vsl = ts(T.sl[:, c], T.xwi[:, c], 2047, None, A.bitwise_and)
         need("v", vv, tb)
         vi = ts(T.idx[:, c], T.vv[:, c], psc[:, 0:1], None, A.add)
+        if s < S - 1:
+            need("v", vsl)
+            vsh = v(g.vector.tensor_copy(T.sh[:, c], T.sl[:, c]))
+            tsl = swap(psb, T.sh[:, ev], T.sh[:, od], T.swh, vsh)
         need("v", vi, chunks[s])
         vrb = v(g.vector.tensor_copy(T.rb[:, wide], T.bt[:, 0:1025 + 1024 * s].indirect(T.idx[:, c])))
+        if s < S - 1:
+            vxk = ts(T.xwk[:, c], T.xwi[:, c], float(K), None, A.add)
         need("v", vrb)
         vtb = v(g.vector.transpose(T.tb[:, wide], T.rb[:, wide]))
         byte = T.tb[:, 256 * s:256 * s + 256:16]
+        need("t", vtb, vswb)
+        tby = swap(psa, T.tb[:, 256 * s:256 * s + 256:32], T.tb[:, 256 * s + 16:256 * s + 256:32], T.swb)
         need("a", vt)
         sy = T.res1[:, c] if s < S - 1 else T.res2[:, 16:32]
         asy = done("a", g.scalar.activation(sy, T.ta[:, 256 * s + 1:256 * s + 256:16], COPY))
         if s + 2 < S:
             chunks.append(chunk(s + 2))
-        if s == 2:
-            need("a", vsw)
-            aswb = done("a", g.scalar.activation(T.swb[:], T.sw[:], COPY))
         if s == S - 2:
             need("g", asy)
             same(T.res1[:], T.back1, "r1")
             need("y", asy)
             g.sync.dma_start(T.back1[rank], T.res1[:]).then_inc(T.sem.dback1, 16)
         if s < S - 1:
-            need("v", vtb, tw)
-            vxi = tt(T.xi[:, 16 * s + 16:16 * s + 32], psb[:, 0:16], byte, A.add)
+            need("v", vtb, tsl)
+            vsf = tt(T.slf[:, nx], psb[:, 0:16], byte, A.add)
+            need("v", vsf)
+            vl = v(g.vector.tensor_copy(T.lst[:, nx], T.slf[:, nx]))
         else:
-            need("t", vtb, aswb)
-            tl = swap(psb, T.tb[:, 256 * s:256 * s + 256:32], T.tb[:, 256 * s + 16:256 * s + 256:32], T.swb)
-            need("v", tl)
-            vlast = tt(T.res2[:, 0:16], psb[:, 0:16], T.xw[:, c], A.add)
+            need("v", tby)
+            vlast = tt(T.res2[:, 0:16], psa[:, 0:16], T.xwi[:, c], A.add)
 
     need("g", vlast, asy)
     same(T.res2[:], T.back2, "r2")

@@ -4,20 +4,18 @@ from concourse.mybir import dt, AluOpType, ActivationFunctionType
 
 SCRATCH = {
     "stgm": ("dram", [4, 128, 64], "int32"), "landm": ("dram", [4, 128, 64], "int32"),
-    "stgs": ("dram", [4, 128, 32], "float32"), "lands": ("dram", [4, 128, 32], "float32"),
+    "stgs": ("dram", [4, 128, 32], "int32"), "lands": ("dram", [4, 128, 32], "int32"),
     "back1": ("dram", [4, 128, 64], "float32"), "back2": ("dram", [4, 128, 32], "float32"),
-    "win": ("sbuf", [128, 4096], "int32"), "pool": ("sbuf", [128, 5120], "float32"), "bt": ("sbuf", [128, 5136], "bfloat16"),
-    "zero": ("sbuf", [128, 512], "bfloat16"), "padz": ("sbuf", [128, 32], "float32"),
-    "pl": ("sbuf", [128, 10, 16], "int32"), "pa": ("sbuf", [128, 10, 16], "int32"), "pb": ("sbuf", [128, 10, 16], "int32"),
-    "pc": ("sbuf", [128, 10, 16], "float32"), "pi3": ("sbuf", [128, 10, 32], "float32"),
-    "pt": ("sbuf", [128, 320], "float32"), "order": ("sbuf", [128, 320], "uint16"),
+    "win": ("sbuf", [128, 5120], "int32"), "bt": ("sbuf", [128, 5136], "bfloat16"),
+    "pl": ("sbuf", [128, 8, 16], "int32"), "pa": ("sbuf", [128, 8, 16], "int32"), "pb": ("sbuf", [128, 8, 16], "int32"),
+    "ha": ("sbuf", [128, 8, 32], "float16"), "hb": ("sbuf", [128, 8, 32], "float16"), "ident": ("sbuf", [128, 256], "float16"),
+    "order": ("sbuf", [128, 320], "uint16"), "pso": ("psum", [128, 512], "float32"),
     "dm": ("sbuf", [128, 128], "float32"), "rowkey": ("sbuf", [128, 256], "float32"),
     "coli": ("sbuf", [128, 8], "int32"), "colj": ("sbuf", [128, 8], "int32"), "colk": ("sbuf", [128, 8], "float32"),
     "flags": ("sbuf", [128, 4], "float32"), "swh": ("sbuf", [128, 512], "float16"), "swb": ("sbuf", [128, 512], "bfloat16"),
     "c16": ("sbuf", [128, 128], "bfloat16"),
     "tri": ("sbuf", [128, 512], "bfloat16"), "allm": ("sbuf", [128, 128], "bfloat16"), "ones": ("sbuf", [128, 16], "bfloat16"),
-    "x0": ("sbuf", [128, 16], "float32"), "x0i": ("sbuf", [128, 16], "int32"), "sl0": ("sbuf", [128, 16], "int32"),
-    "sh0": ("sbuf", [128, 16], "float16"),
+    "x0": ("sbuf", [128, 16], "int32"), "sl0": ("sbuf", [128, 16], "int32"), "sh0": ("sbuf", [128, 16], "float16"),
     "xf": ("sbuf", [128, 80], "float32"), "slf": ("sbuf", [128, 80], "float32"),
     "lst": ("sbuf", [128, 80], "uint16"), "ra": ("sbuf", [128, 1280], "float32"), "ta": ("sbuf", [128, 1280], "float32"),
     "gg": ("sbuf", [128, 80], "int32"), "yh": ("sbuf", [128, 80], "int32"), "q2": ("sbuf", [128, 80], "float32"),
@@ -32,7 +30,7 @@ SCRATCH = {
     "psb0": ("psum", [128, 512], "float32"), "psb1": ("psum", [128, 512], "float32"),
     "psc0": ("psum", [128, 512], "float32"), "psc1": ("psum", [128, 512], "float32"),
 }
-SEMAPHORES = ["v", "a", "t", "k", "dstage", "dpad", "down", "down2", "dpl", "gcast", "dwin", "dx", "dpool", "rs", "rm", "r1",
+SEMAPHORES = ["v", "a", "t", "k", "dstm", "dsts", "downm", "downs", "dpl", "dwin", "dx", "dpool", "rs", "rm", "r1",
               "r2", "loc", "dback1", "dback2", "dout", "dout2"]
 
 
@@ -45,7 +43,7 @@ def rank_program(g, core, T, topo):
     S, L = 5, 256
     others = [c for c in T.cores if c != core]
     K = 2047 * 2048
-    FILL = 3328
+    FILL = 4608
 
     queues = {"g": g, "v": g.vector, "a": g.scalar, "t": g.tensor, "y": g.sync}
     count = {"v": 0, "a": 0, "t": 0, "k": 0}
@@ -96,87 +94,95 @@ def rank_program(g, core, T, topo):
         g.remote_dma_fused([RemoteDMATransfer(srcs=[src], dsts=[land[rank] for c in others], dst_ids=[dst(c) for c in others],
                                               dma_engine_mask=bits(es), remote_sem=T.sem[sem])], local_sem=T.sem.loc)
 
-    g.dma_start(T.stgs[:, 0:80, :], T.stock[:]).then_inc(T.sem.gcast, 16)
-    g.dma_start(T.stgs[:, 80:96, :], T.states[:]).then_inc(T.sem.gcast, 16)
-    g.sync.dma_start(T.stgm[:, 0:64, :], T.models[:]).then_inc(T.sem.dstage, 16)
-    g.sync.dma_start(T.stgm[:, 64:128, :], T.letters[:]).then_inc(T.sem.dstage, 16)
-    g.sync.dma_start(T.landm[rank, 0:64, :], T.models[2 * rank:2 * rank + 2, :]).then_inc(T.sem.down, 16)
-    g.sync.dma_start(T.landm[rank, 64:128, :], T.letters[2 * rank:2 * rank + 2, :]).then_inc(T.sem.down, 16)
-    vpad = v(g.vector.memset(T.padz[:], 0.0))
-    need("a", vpad)
-    g.scalar.dma_start(T.stgs[:, 96:128, :], T.padz[:]).then_inc(T.sem.dpad, 16)
-    for a in range(4):
-        g.scalar.dma_start(T.pl[32 * a:32 * a + 32, :, :], T.places[2 * rank + a // 2, :]).then_inc(T.sem.dpl, 16)
-    dpl = ("dpl", 64)
+    own = slice(2 * rank, 2 * rank + 2)
+    g.scalar.dma_start(T.stgs[:, 0:80, :], T.stock[:]).then_inc(T.sem.dsts, 16)
+    g.scalar.dma_start(T.stgs[:, 80:96, :], T.states[:]).then_inc(T.sem.dsts, 16)
+    g.scalar.dma_start(T.stgs[:, 96:128, :], T.letters[0:2, :]).then_inc(T.sem.dsts, 16)
+    g.sync.dma_start(T.stgm[:, 0:64, :], T.models[:]).then_inc(T.sem.dstm, 16)
+    g.sync.dma_start(T.stgm[:, 64:128, :], T.letters[:]).then_inc(T.sem.dstm, 16)
+    for sg in range(2):
+        g.scalar.dma_start(T.pl[0:80, 4 * sg:4 * sg + 4, :], T.places[2 * rank + sg, :]).then_inc(T.sem.dpl, 16)
+    g.sync.dma_start(T.landm[rank, 0:64, :], T.models[own, :]).then_inc(T.sem.downm, 16)
+    g.sync.dma_start(T.landm[rank, 64:128, :], T.letters[own, :]).then_inc(T.sem.downm, 16)
+    g.scalar.dma_start(T.lands[rank, 0:80, :], T.stock[own, :]).then_inc(T.sem.downs, 16)
+    g.scalar.dma_start(T.lands[rank, 80:96, :], T.states[own, :]).then_inc(T.sem.downs, 16)
 
-    kwin = done("k", g.iota(T.win[:, FILL:4096], [[0, 4096 - FILL]], 0, 0))
     done("k", g.iota(T.coli[:, 0:4], [[-16, 4]], 64, 1))
-    k1 = done("k", g.iota(T.coli[:, 4:8], [[0, 4]], 0, 1))
-
-    need("g", ("gcast", 32), ("dpad", 16))
-    spread(T.stgs, T.lands, "rs")
-    need("g", ("dstage", 32))
-    spread(T.stgm, T.landm, "rm")
+    done("k", g.iota(T.coli[:, 4:8], [[0, 4]], 0, 1))
     k2 = done("k", g.iota(T.dm[:], [[1, 128]], 0, -1, allow_small_or_imprecise_dtypes=True))
+    kwin = done("k", g.iota(T.win[:, FILL:5120], [[0, 5120 - FILL]], 0, 0))
+    need("g", ("dsts", 48))
+    spread(T.stgs, T.lands, "rs")
+    need("g", ("dstm", 32))
+    spread(T.stgm, T.landm, "rm")
     k3 = done("k", g.iota(T.rowkey[:], [[0, 4], [1, 64]], 0, 0, allow_small_or_imprecise_dtypes=True))
 
-    vz = v(g.vector.memset(T.zero[:], 0.0))
-    vwin = v(g.vector.memset(T.win[:, 0:FILL], 0))
+    mm = g.tensor.matmul
+
     v(g.vector.memset(T.bt[:, 0:1], 0.0))
     v(g.vector.memset(T.ones[:], 1.0))
     vc16 = v(g.vector.memset(T.c16[:], 16.0))
-    need("v", dpl)
-    p1 = ts(T.pa[:], T.pl[:], 3, None, A.bitwise_and)
-    p2 = ts(T.pb[:], T.pl[:], 2, None, A.arith_shift_right)
+    vwin = v(g.vector.memset(T.win[:, 0:FILL], 0))
+    need("v", ("dpl", 32))
+    p1 = ts(T.pa[0:80, :, :], T.pl[0:80, :, :], 3, None, A.bitwise_and)
+    p2 = ts(T.pb[0:80, :, :], T.pl[0:80, :, :], 2, None, A.arith_shift_right)
+    need("v", k2)
+    ts(T.ident[:, 0:128], T.dm[:], 0.0, 1280.0, A.is_equal, A.mult)
+    ts(T.ident[:, 128:256], T.dm[:], 0.0, None, A.is_equal)
     need("v", p1)
-    p3 = ts(T.pc[:], T.pa[:], 1280.0, None, A.mult)
-    need("v", k1)
+    for ga in range(2):
+        v(g.vector.tensor_copy(T.ha[0:80, :, 16 * ga:16 * ga + 16], T.pa[0:80, :, :]))
+    need("v", p2)
+    for ga in range(2):
+        vh = v(g.vector.tensor_copy(T.hb[0:80, :, 16 * ga:16 * ga + 16], T.pb[0:80, :, :]))
+    need("t", vh)
+    for a in range(4):
+        for q in range(4):
+            o = T.pso[32 * a:32 * a + 32, 80 * q:80 * q + 80]
+            mm(o, T.ha[0:80, 4 * (a // 2) + q, :], T.ident[0:80, 0:80], True, False)
+            call = mm(o, T.hb[0:80, 4 * (a // 2) + q, :], T.ident[0:80, 128:208], False, True)
+    to = done("t", call)
     ts(T.colj[:, 0:4], T.coli[:, 0:4], 63, None, A.bitwise_and)
     c2 = ts(T.colj[:, 4:8], T.coli[:, 4:8], 16, None, A.bitwise_and)
-    need("v", p3)
-    tt(T.pi3[:, :, 0:16], T.pb[:], T.pc[:], A.add)
-    p4 = tt(T.pi3[:, :, 16:32], T.pb[:], T.pc[:], A.add)
+    ts(T.flags[:, 2:3], T.coli[:, 4:5], 64.0, None, A.is_lt)
+    ts(T.flags[:, 3:4], T.coli[:, 4:5], 64.0, None, A.is_ge)
     need("v", c2)
     ts(T.flags[:, 0:1], T.colj[:, 4:5], 0.0, None, A.is_equal)
     ts(T.flags[:, 1:2], T.colj[:, 4:5], 16.0, None, A.is_equal)
-    ts(T.flags[:, 2:3], T.coli[:, 4:5], 64.0, None, A.is_lt)
-    ts(T.flags[:, 3:4], T.coli[:, 4:5], 64.0, None, A.is_ge)
     c3 = v(g.vector.tensor_copy(T.colk[:, 0:4], T.colj[:, 0:4]))
-    need("v", p4)
-    for b in range(10):
-        p5 = v(g.vector.transpose(T.pt[:, 32 * b:32 * b + 32], T.pi3[:, b, :]))
-    need("v", p5)
-    for b in range(10):
-        vorder = v(g.vector.tensor_copy(T.order[:, b:320:10], T.pt[:, 32 * b:32 * b + 32]))
-    need("v", k2, c3)
+    need("v", c3)
     for i, (d, f) in enumerate(((0.0, 0), (16.0, 0), (-16.0, 1), (0.0, 1))):
         vsw = ts(T.swh[:, 128 * i:128 * i + 128], T.dm[:], d, T.flags[:, f:f + 1], A.is_equal, A.mult)
+    need("v", to)
+    for q in range(4):
+        vorder = v(g.vector.tensor_copy(T.order[:, q:320:4], T.pso[:, 80 * q:80 * q + 80]))
 
-    need("a", vz)
-    for i in range(10):
-        apool = done("a", g.scalar.activation(T.pool[:, 512 * i:512 * i + 512], T.zero[:], COPY))
-    need("y", ("gcast", 32))
-    g.sync.dma_start(T.lands[rank, 0:96, :], T.stgs[rank, 0:96, :]).then_inc(T.sem.down2, 16)
-    need("a", ("down2", 16), ("rs", 6))
-    for sg in range(2):
-        g.scalar.dma_start(T.x0[64 * sg:64 * sg + 64, :], T.lands[:, 80 + 8 * sg:88 + 8 * sg, :]).then_inc(T.sem.dx, 16)
-    need("a", apool)
-    for i in range(8):
+    def load_pool(queue, i):
         sg = i // 4
-        g.scalar.dma_start(T.pool[16 * i:16 * i + 1, :], T.lands[:, 40 * sg:40 * sg + 40, :]).then_inc(T.sem.dpool, 16)
-    need("y", ("down", 32), ("rm", 6), vwin, kwin)
-    for kind in range(2):
+        queue.dma_start(T.win[16 * i + 2:16 * i + 3, :], T.lands[:, 40 * sg:40 * sg + 40, :]).then_inc(T.sem.dpool, 16)
+
+    def load_tables(queue, kind):
         for ga in range(2):
             for sg in range(2):
                 p = 64 * sg + 16 * ga + kind
-                g.sync.dma_start(T.win[p:p + 33:32, :], T.landm[:, 64 * kind + 32 * sg:64 * kind + 32 * sg + 32, :]).then_inc(T.sem.dwin, 16)
+                queue.dma_start(T.win[p:p + 33:32, 0:4096], T.landm[:, 64 * kind + 32 * sg:64 * kind + 32 * sg + 32, :]).then_inc(T.sem.dwin, 16)
 
-    mm = g.tensor.matmul
+    need("a", ("downs", 32), ("rs", 6))
+    for sg in range(2):
+        g.scalar.dma_start(T.x0[64 * sg:64 * sg + 64, :], T.lands[:, 80 + 8 * sg:88 + 8 * sg, :]).then_inc(T.sem.dx, 16)
+    need("a", vwin, kwin)
+    need("y", ("downs", 32), ("rs", 6), vwin, kwin)
+    for i in range(4):
+        load_pool(g.scalar, i)
+        load_pool(g.sync, 4 + i)
+    need("y", ("downm", 32), ("rm", 6))
+    load_tables(g.sync, 0)
+    need("a", ("downm", 32), ("rm", 6))
+    load_tables(g.scalar, 1)
 
     def swap(ps, even, odd, mats, offset=None):
         if offset is not None:
             mm(ps[:, 1:16:2], T.c16[:], T.ones[:, 0:8], True, False)
-        if offset is not None:
             need("t", offset)
         mm(ps[:, 1:16:2], mats[:, 256:384], even, offset is None, False)
         mm(ps[:, 1:16:2], mats[:, 384:512], odd, False, True)
@@ -184,13 +190,11 @@ def rank_program(g, core, T, topo):
         return done("t", mm(ps[:, 0:16:2], mats[:, 128:256], odd, False, True))
 
     def chunk(s):
-        return done("a", g.scalar.activation(T.bt[:, 1 + 1024 * s:1025 + 1024 * s], T.pool[:].indirect(T.order[:, 64 * s:64 * s + 64]), COPY))
+        return done("a", g.scalar.activation(T.bt[:, 1 + 1024 * s:1025 + 1024 * s], T.win[:].indirect(T.order[:, 64 * s:64 * s + 64]), COPY))
 
     need("v", ("dx", 32))
-    n1 = v(g.vector.tensor_copy(T.x0i[:], T.x0[:]))
+    n2 = ts(T.sl0[:], T.x0[:], 2047, None, A.bitwise_and)
     vxs = ts(T.xf[:, 0:16], T.x0[:], float(K), None, A.add)
-    need("v", n1)
-    n2 = ts(T.sl0[:], T.x0i[:], 2047, None, A.bitwise_and)
     need("v", n2)
     n3 = v(g.vector.tensor_copy(T.sh0[:], T.sl0[:]))
     need("t", vc16, vsw)
@@ -207,7 +211,7 @@ def rank_program(g, core, T, topo):
     need("v", tx)
     vl = v(g.vector.tensor_copy(T.lst[:, 0:16], T.psb1[:, 0:16]))
 
-    need("a", ("dpool", 128), vorder)
+    need("a", ("dpool", 128), ("dwin", 128), vorder)
     chunks = [chunk(0), chunk(1)]
     for s in range(S):
         c = slice(16 * s, 16 * s + 16)
@@ -218,8 +222,8 @@ def rank_program(g, core, T, topo):
         psa, psb, psc = T["psa%d" % (s % 2)], T["psb%d" % (s % 2)], T["psc%d" % (s % 2)]
         for q in range(s):
             mm(psc[:, 0:1], T.allm[:], T.cs[:, 16 * q + 15:16 * q + 16], q == 0, False)
-        need("v", vl, ("dwin", 128))
-        vr = v(g.vector.tensor_copy(T.ra[:, wide], T.win[:].indirect(T.lst[:, c])))
+        need("v", vl, ("dpool", 128), ("dwin", 128))
+        vr = v(g.vector.tensor_copy(T.ra[:, wide], T.win[:, 0:4096].indirect(T.lst[:, c])))
         if s:
             need("v", tby)
             vxs = tt(T.xf[:, c], T["psa%d" % ((s - 1) % 2)][:, 0:16], T.xwk[:, 16 * s - 16:16 * s], A.add)
@@ -265,9 +269,9 @@ def rank_program(g, core, T, topo):
             vxk = ts(T.xwk[:, c], T.xwi[:, c], float(K), None, A.add)
         need("v", vrb)
         vtb = v(g.vector.transpose(T.tb[:, wide], T.rb[:, wide]))
-        byte = T.tb[:, 256 * s:256 * s + 256:16]
+        byte = T.tb[:, 256 * s + 2:256 * s + 256:16]
         need("t", vtb, vswb)
-        tby = swap(psa, T.tb[:, 256 * s:256 * s + 256:32], T.tb[:, 256 * s + 16:256 * s + 256:32], T.swb)
+        tby = swap(psa, T.tb[:, 256 * s + 2:256 * s + 256:32], T.tb[:, 256 * s + 18:256 * s + 256:32], T.swb)
         need("a", vt)
         sy = T.res1[:, c] if s < S - 1 else T.res2[:, 16:32]
         asy = done("a", g.scalar.activation(sy, T.ta[:, 256 * s + 1:256 * s + 256:16], COPY))

@@ -13,8 +13,9 @@ SCRATCH = {
     "dm": ("sbuf", [128, 128], "float32"), "rowkey": ("sbuf", [128, 256], "float32"),
     "coli": ("sbuf", [128, 8], "int32"), "colj": ("sbuf", [128, 8], "int32"), "colk": ("sbuf", [128, 8], "float32"),
     "flags": ("sbuf", [128, 4], "float32"), "swh": ("sbuf", [128, 512], "float16"), "swb": ("sbuf", [128, 512], "bfloat16"),
-    "c16": ("sbuf", [128, 128], "bfloat16"),
+    "c16": ("sbuf", [128, 128], "bfloat16"), "c16h": ("sbuf", [128, 128], "float16"), "kh": ("sbuf", [128, 16], "float16"),
     "tri": ("sbuf", [128, 512], "bfloat16"), "allm": ("sbuf", [128, 128], "bfloat16"), "ones": ("sbuf", [128, 16], "bfloat16"),
+    "sgn": ("sbuf", [128, 256], "bfloat16"),
     "x0": ("sbuf", [128, 16], "int32"), "sl0": ("sbuf", [128, 16], "int32"), "sh0": ("sbuf", [128, 16], "float16"),
     "xf": ("sbuf", [128, 80], "float32"), "slf": ("sbuf", [128, 80], "float32"),
     "lst": ("sbuf", [128, 80], "uint16"), "ra": ("sbuf", [128, 1280], "float32"), "ta": ("sbuf", [128, 1280], "float32"),
@@ -22,7 +23,7 @@ SCRATCH = {
     "rr": ("sbuf", [128, 80], "float32"),
     "t2": ("sbuf", [128, 80], "float32"), "xn": ("sbuf", [128, 80], "float32"), "wr": ("sbuf", [128, 80], "bfloat16"),
     "cs": ("sbuf", [128, 80], "bfloat16"), "mm": ("sbuf", [128, 80], "float32"), "xwi": ("sbuf", [128, 80], "int32"),
-    "xwk": ("sbuf", [128, 80], "float32"), "sl": ("sbuf", [128, 80], "int32"), "sh": ("sbuf", [128, 80], "float16"),
+    "sl": ("sbuf", [128, 80], "int32"), "sh": ("sbuf", [128, 80], "float16"),
     "uu": ("sbuf", [128, 80], "float32"), "vv": ("sbuf", [128, 80], "float32"), "idx": ("sbuf", [128, 80], "uint16"),
     "rb": ("sbuf", [128, 1280], "bfloat16"), "tb": ("sbuf", [128, 1280], "bfloat16"),
     "res1": ("sbuf", [128, 64], "float32"), "res2": ("sbuf", [128, 32], "float32"),
@@ -39,7 +40,8 @@ def rank_program(g, core, T, topo):
     if rank is None:
         return
     A = AluOpType
-    COPY = ActivationFunctionType.Copy
+    AF = ActivationFunctionType
+    COPY = AF.Copy
     S, L = 5, 256
     others = [c for c in T.cores if c != core]
     K = 2047 * 2048
@@ -70,6 +72,9 @@ def rank_program(g, core, T, topo):
 
     def tt(out, a, b, op):
         return v(g.vector.tensor_tensor(out, a, b, op))
+
+    def act(*args, **kw):
+        return done("a", g.scalar.activation(*args, **kw))
 
     def dst(c):
         rid, pid, _ = topo.addr(c)
@@ -120,7 +125,7 @@ def rank_program(g, core, T, topo):
     mm = g.tensor.matmul
 
     v(g.vector.memset(T.bt[:, 0:1], 0.0))
-    v(g.vector.memset(T.ones[:], 1.0))
+    v1 = v(g.vector.memset(T.ones[:], 1.0))
     vc16 = v(g.vector.memset(T.c16[:], 16.0))
     vwin = v(g.vector.memset(T.win[:, 0:FILL], 0))
     need("v", ("dpl", 32))
@@ -149,7 +154,8 @@ def rank_program(g, core, T, topo):
     need("v", c2)
     ts(T.flags[:, 0:1], T.colj[:, 4:5], 0.0, None, A.is_equal)
     ts(T.flags[:, 1:2], T.colj[:, 4:5], 16.0, None, A.is_equal)
-    c3 = v(g.vector.tensor_copy(T.colk[:, 0:4], T.colj[:, 0:4]))
+    v(g.vector.tensor_copy(T.colk[:, 0:4], T.colj[:, 0:4]))
+    c3 = ts(T.colk[:, 4:8], T.colj[:, 0:4], -1.0, None, A.mult)
     need("v", c3)
     for i, (d, f) in enumerate(((0.0, 0), (16.0, 0), (-16.0, 1), (0.0, 1))):
         vsw = ts(T.swh[:, 128 * i:128 * i + 128], T.dm[:], d, T.flags[:, f:f + 1], A.is_equal, A.mult)
@@ -180,17 +186,23 @@ def rank_program(g, core, T, topo):
     need("a", ("downm", 32), ("rm", 6))
     load_tables(g.scalar, 1)
 
-    def swap(ps, even, odd, mats, offset=None):
-        if offset is not None:
-            mm(ps[:, 1:16:2], T.c16[:], T.ones[:, 0:8], True, False)
-            need("t", offset)
-        mm(ps[:, 1:16:2], mats[:, 256:384], even, offset is None, False)
-        mm(ps[:, 1:16:2], mats[:, 384:512], odd, False, True)
-        mm(ps[:, 0:16:2], mats[:, 0:128], even, True, False)
-        return done("t", mm(ps[:, 0:16:2], mats[:, 128:256], odd, False, True))
+    def swap(ps, even, odd, mats, tokens, odd_const=None, even_const=None):
+        for cols, const, m in ((slice(1, 16, 2), odd_const, 256), (slice(0, 16, 2), even_const, 0)):
+            if const is not None:
+                mm(ps[:, cols], const[0], const[1], True, False)
+            need("t", *tokens)
+            mm(ps[:, cols], mats[:, m:m + 128], even, const is None, False)
+            call = mm(ps[:, cols], mats[:, m + 128:m + 256], odd, False, True)
+        return done("t", call)
 
-    def chunk(s):
-        return done("a", g.scalar.activation(T.bt[:, 1 + 1024 * s:1025 + 1024 * s], T.win[:].indirect(T.order[:, 64 * s:64 * s + 64]), COPY))
+    second = (T.c16[:], T.ones[:, 0:8])
+    plus_k = (T.c16h[:], T.kh[:, 0:8])
+    place = [0]
+
+    def order_bytes(n):
+        p = place[0]
+        place[0] = p + n
+        return act(T.bt[:, 1 + p:1 + p + n], T.win[:].indirect(T.order[:, p // 16:(p + n) // 16]), COPY)
 
     need("v", ("dx", 32))
     n2 = ts(T.sl0[:], T.x0[:], 2047, None, A.bitwise_and)
@@ -198,41 +210,69 @@ def rank_program(g, core, T, topo):
     need("v", n2)
     n3 = v(g.vector.tensor_copy(T.sh0[:], T.sl0[:]))
     need("t", vc16, vsw)
-    tx = swap(T.psb1, T.sh0[:, 0:16:2], T.sh0[:, 1:16:2], T.swh, n3)
+    tx = swap(T.psb1, T.sh0[:, 0:16:2], T.sh0[:, 1:16:2], T.swh, (n3,), second)
     need("v", k3)
-    for r in range(4):
+    for r in range(2):
         for b in range(2):
             o = 64 - 16 * r + 64 * b
-            ts(T.tri[:, 128 * r + 64 * b:128 * r + 64 * b + 64], T.rowkey[:, o:o + 64], T.colk[:, r:r + 1], T.flags[:, 2 + b:3 + b], A.is_gt, A.mult)
+            vtri = ts(T.tri[:, 128 * r + 64 * b:128 * r + 64 * b + 64], T.rowkey[:, o:o + 64], T.colk[:, r:r + 1], T.flags[:, 2 + b:3 + b], A.is_gt, A.mult)
+    need("a", k3, c3)
+    for r in range(2, 4):
+        o = 64 - 16 * r
+        asg = act(T.sgn[:, 128 * r - 256:128 * r - 128], T.rowkey[:, o:o + 128], AF.Sign, bias=T.colk[:, 4 + r:5 + r])
     for b in range(2):
-        vtri = ts(T.allm[:, 64 * b:64 * b + 64], T.rowkey[:, 0:64], 0.0, T.flags[:, 2 + b:3 + b], A.mult, A.add)
+        act(T.allm[:, 64 * b:64 * b + 64], T.rowkey[:, 0:64], AF.Identity, bias=T.flags[:, 2 + b:3 + b], scale=0.0)
+    need("a", asg)
+    for r in range(2, 4):
+        for b in range(2):
+            atri = act(T.tri[:, 128 * r + 64 * b:128 * r + 64 * b + 64], T.sgn[:, 128 * r - 256 + 64 * b:128 * r - 192 + 64 * b], AF.Relu, scale=T.flags[:, 2 + b:3 + b])
     need("v", vsw)
-    vswb = v(g.vector.tensor_copy(T.swb[:], T.swh[:]))
+    v(g.vector.tensor_copy(T.swb[:], T.swh[:]))
+    need("v", v1, vc16)
+    v(g.vector.tensor_copy(T.c16h[:], T.c16[:]))
+    vswb = ts(T.kh[:], T.ones[:], 2047.0, None, A.mult)
     need("v", tx)
     vl = v(g.vector.tensor_copy(T.lst[:, 0:16], T.psb1[:, 0:16]))
 
     need("a", ("dpool", 128), ("dwin", 128), vorder)
-    chunks = [chunk(0), chunk(1)]
+    have = order_bytes(1024)
+    before = (0, 704, 704, 704, 704)
+    after = (320, 320, 320, 320, 0)
     for s in range(S):
         c = slice(16 * s, 16 * s + 16)
         ev = slice(16 * s, 16 * s + 16, 2)
         od = slice(16 * s + 1, 16 * s + 16, 2)
         nx = slice(16 * s + 16, 16 * s + 32)
-        wide = slice(256 * s, 256 * s + 256)
+        w0 = 256 * s
         psa, psb, psc = T["psa%d" % (s % 2)], T["psb%d" % (s % 2)], T["psc%d" % (s % 2)]
+
+        def cut(n):
+            m = 16 * s + n
+            return slice(16 * s, m), slice(m, 16 * s + 16), slice(w0, 16 * m), slice(16 * m, w0 + 256)
+
+        if s:
+            need("t", atri)
         for q in range(s):
             mm(psc[:, 0:1], T.allm[:], T.cs[:, 16 * q + 15:16 * q + 16], q == 0, False)
         need("v", vl, ("dpool", 128), ("dwin", 128))
-        vr = v(g.vector.tensor_copy(T.ra[:, wide], T.win[:, 0:4096].indirect(T.lst[:, c])))
+        tables = T.win[:, 0:4096]
+        clo, chi, lo, hi = cut(6 if s else 16)
+        vr = v(g.vector.tensor_copy(T.ra[:, lo], tables.indirect(T.lst[:, clo])))
         if s:
+            need("a", vl)
+            ar = act(T.ra[:, hi], tables.indirect(T.lst[:, chi]), COPY)
+            have = order_bytes(before[s])
             need("v", tby)
-            vxs = tt(T.xf[:, c], T["psa%d" % ((s - 1) % 2)][:, 0:16], T.xwk[:, 16 * s - 16:16 * s], A.add)
+            vxs = tt(T.xf[:, c], T["psa%d" % ((s - 1) % 2)][:, 0:16], T.xwi[:, 16 * s - 16:16 * s], A.add)
         xs = T.xf[:, c]
         need("v", vr)
-        vt = v(g.vector.transpose(T.ta[:, wide], T.ra[:, wide]))
-        e = T.ta[:, 256 * s:256 * s + 256:16]
+        vt = v(g.vector.transpose(T.ta[:, lo], T.ra[:, lo]))
+        e = T.ta[:, w0:w0 + 256:16]
         need("v", vxs)
         ts(T.yh[:, c], xs, 1.0 / 2048, 0.500244140625, A.mult, A.add)
+        if s:
+            need("v", ar)
+            vt = v(g.vector.transpose(T.ta[:, hi], T.ra[:, hi]))
         need("v", vt)
         vg = ts(T.gg[:, c], e, 1.0 / 2048, -2047.499755859375, A.mult, A.add)
         vq = tt(T.q2[:, c], xs, e, A.subtract)
@@ -262,21 +302,26 @@ def rank_program(g, core, T, topo):
         if s < S - 1:
             need("v", vsl)
             vsh = v(g.vector.tensor_copy(T.sh[:, c], T.sl[:, c]))
-            tsl = swap(psb, T.sh[:, ev], T.sh[:, od], T.swh, vsh)
-        need("v", vi, chunks[s])
-        vrb = v(g.vector.tensor_copy(T.rb[:, wide], T.bt[:, 0:1025 + 1024 * s].indirect(T.idx[:, c])))
-        if s < S - 1:
-            vxk = ts(T.xwk[:, c], T.xwi[:, c], float(K), None, A.add)
+            tsl = swap(psb, T.sh[:, ev], T.sh[:, od], T.swh, (vsh,), second)
+        table = T.bt[:, 0:1025 + 1024 * s]
+        clo, chi, lo, hi = cut(8)
+        need("v", vi, have)
+        vrb = v(g.vector.tensor_copy(T.rb[:, lo], table.indirect(T.idx[:, clo])))
+        need("a", vi, have)
+        arb = act(T.rb[:, hi], table.indirect(T.idx[:, chi]), COPY)
         need("v", vrb)
-        vtb = v(g.vector.transpose(T.tb[:, wide], T.rb[:, wide]))
-        byte = T.tb[:, 256 * s + 2:256 * s + 256:16]
-        need("t", vtb, vswb)
-        tby = swap(psa, T.tb[:, 256 * s + 2:256 * s + 256:32], T.tb[:, 256 * s + 18:256 * s + 256:32], T.swb)
+        v(g.vector.transpose(T.tb[:, lo], T.rb[:, lo]))
+        need("v", arb)
+        vtb = v(g.vector.transpose(T.tb[:, hi], T.rb[:, hi]))
+        byte = T.tb[:, w0 + 2:w0 + 256:16]
+        need("t", vswb)
+        const = plus_k if s < S - 1 else None
+        tby = swap(psa, T.tb[:, w0 + 2:w0 + 256:32], T.tb[:, w0 + 18:w0 + 256:32], T.swb, (vtb,), const, const)
         need("a", vt)
         sy = T.res1[:, c] if s < S - 1 else T.res2[:, 16:32]
-        asy = done("a", g.scalar.activation(sy, T.ta[:, 256 * s + 1:256 * s + 256:16], COPY))
-        if s + 2 < S:
-            chunks.append(chunk(s + 2))
+        asy = act(sy, T.ta[:, w0 + 1:w0 + 256:16], COPY)
+        if after[s]:
+            have = order_bytes(after[s])
         if s == S - 2:
             need("g", asy)
             same(T.res1[:], T.back1, "r1")

@@ -5,34 +5,39 @@ from concourse.mybir import dt, AluOpType, ActivationFunctionType
 SCRATCH = {
     "stgm": ("dram", [4, 128, 64], "int32"), "landm": ("dram", [4, 128, 64], "int32"),
     "stgs": ("dram", [4, 128, 32], "int32"), "lands": ("dram", [4, 128, 32], "int32"),
-    "back1": ("dram", [4, 128, 64], "float32"), "back2": ("dram", [4, 128, 32], "float32"),
+    "back1": ("dram", [4, 128, 64], "float32"), "back2": ("dram", [4, 128, 16], "float32"), "back3": ("dram", [4, 128, 16], "float32"),
     "win": ("sbuf", [128, 5120], "int32"), "bt": ("sbuf", [128, 5136], "bfloat16"),
+    "qa": ("sbuf", [128, 256], "bfloat16"), "qb": ("sbuf", [128, 768], "bfloat16"),
     "pl": ("sbuf", [128, 8, 16], "int32"), "pa": ("sbuf", [128, 8, 16], "int32"), "pb": ("sbuf", [128, 8, 16], "int32"),
-    "ha": ("sbuf", [128, 8, 32], "float16"), "hb": ("sbuf", [128, 8, 32], "float16"), "ident": ("sbuf", [128, 256], "float16"),
-    "order": ("sbuf", [128, 320], "uint16"), "pso": ("psum", [128, 512], "float32"),
+    "ha": ("sbuf", [128, 8, 48], "float16"), "hb": ("sbuf", [128, 8, 48], "float16"), "zz": ("sbuf", [128, 8, 16], "bfloat16"),
+    "sraw": ("sbuf", [128, 4, 32], "float32"), "sela": ("sbuf", [128, 4, 32], "float16"), "selb": ("sbuf", [128, 4, 32], "float16"),
+    "order": ("sbuf", [128, 128], "uint16"), "pso": ("psum", [128, 512], "float32"),
     "dm": ("sbuf", [128, 128], "float32"), "rowkey": ("sbuf", [128, 256], "float32"),
     "coli": ("sbuf", [128, 8], "int32"), "colj": ("sbuf", [128, 8], "int32"), "colk": ("sbuf", [128, 8], "float32"),
+    "colp": ("sbuf", [128, 8], "int32"), "part": ("sbuf", [128, 8], "float32"), "sc": ("sbuf", [128, 4], "float32"),
     "flags": ("sbuf", [128, 4], "float32"), "swh": ("sbuf", [128, 512], "float16"), "swb": ("sbuf", [128, 512], "bfloat16"),
     "c16": ("sbuf", [128, 128], "bfloat16"), "c16h": ("sbuf", [128, 128], "float16"), "kh": ("sbuf", [128, 16], "float16"),
     "tri": ("sbuf", [128, 512], "bfloat16"), "allm": ("sbuf", [128, 128], "bfloat16"), "ones": ("sbuf", [128, 16], "bfloat16"),
-    "sgn": ("sbuf", [128, 256], "bfloat16"),
-    "x0": ("sbuf", [128, 16], "int32"), "sl0": ("sbuf", [128, 16], "int32"), "sh0": ("sbuf", [128, 16], "float16"),
+    "two": ("sbuf", [128, 16], "bfloat16"), "odd1": ("sbuf", [128, 16], "bfloat16"), "lift": ("sbuf", [128, 128], "bfloat16"),
+    "sgn": ("sbuf", [128, 512], "bfloat16"),
+    "x0": ("sbuf", [128, 16], "int32"), "sl0": ("sbuf", [128, 16], "int32"), "y0": ("sbuf", [128, 16], "int32"),
+    "sh0": ("sbuf", [128, 16], "float16"),
     "xf": ("sbuf", [128, 80], "float32"), "slf": ("sbuf", [128, 80], "float32"),
     "lst": ("sbuf", [128, 80], "uint16"), "ra": ("sbuf", [128, 1280], "float32"), "ta": ("sbuf", [128, 1280], "float32"),
-    "gg": ("sbuf", [128, 80], "int32"), "yh": ("sbuf", [128, 80], "int32"), "q2": ("sbuf", [128, 80], "float32"),
-    "rr": ("sbuf", [128, 80], "float32"),
-    "t2": ("sbuf", [128, 80], "float32"), "xn": ("sbuf", [128, 80], "float32"), "wr": ("sbuf", [128, 80], "bfloat16"),
+    "yy": ("sbuf", [128, 80], "int32"), "my": ("sbuf", [128, 80], "float32"),
+    "d0": ("sbuf", [128, 320], "float32"), "st": ("sbuf", [128, 320], "float32"),
+    "xn": ("sbuf", [128, 80], "float32"), "wr": ("sbuf", [128, 80], "bfloat16"),
     "cs": ("sbuf", [128, 80], "bfloat16"), "mm": ("sbuf", [128, 80], "float32"), "xwi": ("sbuf", [128, 80], "int32"),
     "sl": ("sbuf", [128, 80], "int32"), "sh": ("sbuf", [128, 80], "float16"),
     "uu": ("sbuf", [128, 80], "float32"), "vv": ("sbuf", [128, 80], "float32"), "idx": ("sbuf", [128, 80], "uint16"),
     "rb": ("sbuf", [128, 1280], "bfloat16"), "tb": ("sbuf", [128, 1280], "bfloat16"),
-    "res1": ("sbuf", [128, 64], "float32"), "res2": ("sbuf", [128, 32], "float32"),
+    "res1": ("sbuf", [128, 64], "float32"), "res2": ("sbuf", [128, 16], "float32"), "res3": ("sbuf", [128, 16], "float32"),
     "psa0": ("psum", [128, 512], "float32"), "psa1": ("psum", [128, 512], "float32"),
     "psb0": ("psum", [128, 512], "float32"), "psb1": ("psum", [128, 512], "float32"),
     "psc0": ("psum", [128, 512], "float32"), "psc1": ("psum", [128, 512], "float32"),
 }
-SEMAPHORES = ["v", "a", "t", "k", "dstm", "dsts", "downm", "downs", "dpl", "dwin", "dx", "dpool", "rs", "rm", "r1",
-              "r2", "loc", "dback1", "dback2", "dout", "dout2"]
+SEMAPHORES = ["v", "a", "t", "k", "dstm", "dsts", "downm", "downs", "dpl", "dfill", "dwin", "dx", "dpool", "dqa", "dqb",
+              "rs", "rm", "r1", "r2", "r3", "loc", "dback1", "dback2", "dback3", "dout", "dout2"]
 
 
 def rank_program(g, core, T, topo):
@@ -45,7 +50,10 @@ def rank_program(g, core, T, topo):
     S, L = 5, 256
     others = [c for c in T.cores if c != core]
     K = 2047 * 2048
-    FILL = 4608
+    FILL = 3520
+    Z = 16
+    MODEL, BYTE = 6, 8
+    BIG = 2.0 ** 23
 
     queues = {"g": g, "v": g.vector, "a": g.scalar, "t": g.tensor, "y": g.sync}
     count = {"v": 0, "a": 0, "t": 0, "k": 0}
@@ -109,248 +117,296 @@ def rank_program(g, core, T, topo):
         g.scalar.dma_start(T.pl[0:80, 4 * sg:4 * sg + 4, :], T.places[2 * rank + sg, :]).then_inc(T.sem.dpl, 16)
     g.sync.dma_start(T.landm[rank, 0:64, :], T.models[own, :]).then_inc(T.sem.downm, 16)
     g.sync.dma_start(T.landm[rank, 64:128, :], T.letters[own, :]).then_inc(T.sem.downm, 16)
-    g.scalar.dma_start(T.lands[rank, 0:80, :], T.stock[own, :]).then_inc(T.sem.downs, 16)
-    g.scalar.dma_start(T.lands[rank, 80:96, :], T.states[own, :]).then_inc(T.sem.downs, 16)
+    g.sync.dma_start(T.lands[rank, 0:80, :], T.stock[own, :]).then_inc(T.sem.downs, 16)
+    g.sync.dma_start(T.lands[rank, 80:96, :], T.states[own, :]).then_inc(T.sem.downs, 16)
+    fills = range(FILL, 5120, 320)
+    for a in fills:
+        g.sync.dma_start(T.win[:, a:a + 320], T.places[:]).then_inc(T.sem.dfill, 16)
+    filled = ("dfill", 16 * len(fills))
 
     done("k", g.iota(T.coli[:, 0:4], [[-16, 4]], 64, 1))
     done("k", g.iota(T.coli[:, 4:8], [[0, 4]], 0, 1))
-    k2 = done("k", g.iota(T.dm[:], [[1, 128]], 0, -1, allow_small_or_imprecise_dtypes=True))
-    kwin = done("k", g.iota(T.win[:, FILL:5120], [[0, 5120 - FILL]], 0, 0))
+    done("k", g.iota(T.sraw[:, :, 0:16], [[0, 4], [1, 16]], 0, -1, allow_small_or_imprecise_dtypes=True))
+    done("k", g.iota(T.sraw[:, :, 16:20], [[4, 4], [1, 4]], 16, -1, allow_small_or_imprecise_dtypes=True))
+    k1 = done("k", g.iota(T.sraw[:, :, 20:32], [[12, 4], [1, 12]], 32, -1, allow_small_or_imprecise_dtypes=True))
     need("g", ("dsts", 48))
     spread(T.stgs, T.lands, "rs")
     need("g", ("dstm", 32))
     spread(T.stgm, T.landm, "rm")
+    k2 = done("k", g.iota(T.dm[:], [[1, 128]], 0, -1, allow_small_or_imprecise_dtypes=True))
     k3 = done("k", g.iota(T.rowkey[:], [[0, 4], [1, 64]], 0, 0, allow_small_or_imprecise_dtypes=True))
+    kd = done("k", g.iota(T.d0[:], [[0, 320]], 1, 0, allow_small_or_imprecise_dtypes=True))
+    need("g", kd)
+    kd = done("k", g.iota(T.d0[:, 0:320:4], [[0, 80]], 0, 0, allow_small_or_imprecise_dtypes=True))
 
     mm = g.tensor.matmul
 
-    v(g.vector.memset(T.bt[:, 0:1], 0.0))
-    v1 = v(g.vector.memset(T.ones[:], 1.0))
-    vc16 = v(g.vector.memset(T.c16[:], 16.0))
-    vwin = v(g.vector.memset(T.win[:, 0:FILL], 0))
+    v(g.vector.memset(T.bt[:, 0:Z], 0.0))
+    vseed = v(g.vector.memset(T.bt[:, 1040:1552], 0.0))
+    v(g.vector.memset(T.win[:, 0:FILL // 2], 0))
+    vz = v(g.vector.memset(T.zz[:], 0.0))
     need("v", ("dpl", 32))
     p1 = ts(T.pa[0:80, :, :], T.pl[0:80, :, :], 3, None, A.bitwise_and)
     p2 = ts(T.pb[0:80, :, :], T.pl[0:80, :, :], 2, None, A.arith_shift_right)
-    need("v", k2)
-    ts(T.ident[:, 0:128], T.dm[:], 0.0, 1280.0, A.is_equal, A.mult)
-    ts(T.ident[:, 128:256], T.dm[:], 0.0, None, A.is_equal)
-    need("v", p1)
-    for ga in range(2):
-        v(g.vector.tensor_copy(T.ha[0:80, :, 16 * ga:16 * ga + 16], T.pa[0:80, :, :]))
+    need("v", vz)
+    for h in (T.ha, T.hb):
+        v(g.vector.tensor_copy(h[0:80, :, 0:16], T.zz[0:80, :, :]))
+        v(g.vector.tensor_copy(h[0:80, :, 32:48], T.zz[0:80, :, :]))
+    need("v", k1)
+    ts(T.sela[:], T.sraw[:], 0.0, 1280.0, A.is_equal, A.mult)
+    ts(T.selb[:], T.sraw[:], 0.0, None, A.is_equal)
     need("v", p2)
-    for ga in range(2):
-        vh = v(g.vector.tensor_copy(T.hb[0:80, :, 16 * ga:16 * ga + 16], T.pb[0:80, :, :]))
+    v(g.vector.tensor_copy(T.ha[0:80, :, 16:32], T.pa[0:80, :, :]))
+    vh = v(g.vector.tensor_copy(T.hb[0:80, :, 16:32], T.pb[0:80, :, :]))
     need("t", vh)
     for a in range(4):
         for q in range(4):
-            o = T.pso[32 * a:32 * a + 32, 80 * q:80 * q + 80]
-            mm(o, T.ha[0:80, 4 * (a // 2) + q, :], T.ident[0:80, 0:80], True, False)
-            call = mm(o, T.hb[0:80, 4 * (a // 2) + q, :], T.ident[0:80, 128:208], False, True)
+            o = T.pso[32 * a:32 * a + 32, q:128:4]
+            for b in range(2):
+                i, w = 2 * (a % 2) + b, slice(16 - 16 * b, 48 - 16 * b)
+                mm(o, T.ha[0:80, 4 * (a // 2) + q, w], T.sela[0:80, i, :], b == 0, False)
+                call = mm(o, T.hb[0:80, 4 * (a // 2) + q, w], T.selb[0:80, i, :], False, b == 1)
     to = done("t", call)
+    vwin = v(g.vector.memset(T.win[:, FILL // 2:FILL], 0))
     ts(T.colj[:, 0:4], T.coli[:, 0:4], 63, None, A.bitwise_and)
     c2 = ts(T.colj[:, 4:8], T.coli[:, 4:8], 16, None, A.bitwise_and)
+    cp = ts(T.colp[:, 0:4], T.coli[:, 4:8], 15, None, A.bitwise_and)
     ts(T.flags[:, 2:3], T.coli[:, 4:5], 64.0, None, A.is_lt)
     ts(T.flags[:, 3:4], T.coli[:, 4:5], 64.0, None, A.is_ge)
     need("v", c2)
-    ts(T.flags[:, 0:1], T.colj[:, 4:5], 0.0, None, A.is_equal)
-    ts(T.flags[:, 1:2], T.colj[:, 4:5], 16.0, None, A.is_equal)
     v(g.vector.tensor_copy(T.colk[:, 0:4], T.colj[:, 0:4]))
     c3 = ts(T.colk[:, 4:8], T.colj[:, 0:4], -1.0, None, A.mult)
-    need("v", c3)
+    ts(T.flags[:, 0:1], T.colj[:, 4:5], 0.0, None, A.is_equal)
+    cf = ts(T.flags[:, 1:2], T.colj[:, 4:5], 16.0, None, A.is_equal)
+    vodd = v(g.vector.memset(T.odd1[:], 0.0))
+    v1 = v(g.vector.memset(T.ones[:], 1.0))
+    vc16 = v(g.vector.memset(T.c16[:], 16.0))
+    need("v", vodd)
+    vodd = v(g.vector.memset(T.odd1[:, 1:16:2], 1.0))
+    need("v", k2, cf)
     for i, (d, f) in enumerate(((0.0, 0), (16.0, 0), (-16.0, 1), (0.0, 1))):
         vsw = ts(T.swh[:, 128 * i:128 * i + 128], T.dm[:], d, T.flags[:, f:f + 1], A.is_equal, A.mult)
-    need("v", to)
-    for q in range(4):
-        vorder = v(g.vector.tensor_copy(T.order[:, q:320:4], T.pso[:, 80 * q:80 * q + 80]))
+
+    need("a", vseed)
+    for a, n in ((1552, 512), (2064, 1024), (3088, 2048)):
+        need("a", ("a", count["a"]))
+        act(T.bt[:, a:a + n], T.bt[:, a - n:a], COPY)
 
     def load_pool(queue, i):
         sg = i // 4
         queue.dma_start(T.win[16 * i + 2:16 * i + 3, :], T.lands[:, 40 * sg:40 * sg + 40, :]).then_inc(T.sem.dpool, 16)
 
-    def load_tables(queue, kind):
+    def load_table(queue, kind, at, sg):
         for ga in range(2):
-            for sg in range(2):
-                p = 64 * sg + 16 * ga + kind
-                queue.dma_start(T.win[p:p + 33:32, 0:4096], T.landm[:, 64 * kind + 32 * sg:64 * kind + 32 * sg + 32, :]).then_inc(T.sem.dwin, 16)
+            p = 64 * sg + 16 * ga + at
+            queue.dma_start(T.win[p:p + 33:32, 0:4096], T.landm[:, 64 * kind + 32 * sg:64 * kind + 32 * sg + 32, :]).then_inc(T.sem.dwin, 16)
 
-    need("a", ("downs", 32), ("rs", 6))
+    need("y", ("downs", 32), ("rs", 6))
     for sg in range(2):
-        g.scalar.dma_start(T.x0[64 * sg:64 * sg + 64, :], T.lands[:, 80 + 8 * sg:88 + 8 * sg, :]).then_inc(T.sem.dx, 16)
-    need("a", vwin, kwin)
-    need("y", ("downs", 32), ("rs", 6), vwin, kwin)
+        g.sync.dma_start(T.x0[64 * sg:64 * sg + 64, :], T.lands[:, 80 + 8 * sg:88 + 8 * sg, :]).then_inc(T.sem.dx, 16)
+    need("y", vwin, filled)
+    need("a", ("downs", 32), ("rs", 6), vwin, filled)
     for i in range(4):
         load_pool(g.scalar, i)
         load_pool(g.sync, 4 + i)
     need("y", ("downm", 32), ("rm", 6))
-    load_tables(g.sync, 0)
     need("a", ("downm", 32), ("rm", 6))
-    load_tables(g.scalar, 1)
+    for kind, at in ((0, 0), (0, 8), (1, 1)):
+        load_table(g.sync, kind, at, 0)
+        load_table(g.scalar, kind, at, 1)
+    loaded = (("dpool", 128), ("dwin", 192))
 
-    def swap(ps, even, odd, mats, tokens, odd_const=None, even_const=None):
-        for cols, const, m in ((slice(1, 16, 2), odd_const, 256), (slice(0, 16, 2), even_const, 0)):
-            if const is not None:
-                mm(ps[:, cols], const[0], const[1], True, False)
-            need("t", *tokens)
-            mm(ps[:, cols], mats[:, m:m + 128], even, const is None, False)
-            call = mm(ps[:, cols], mats[:, m + 128:m + 256], odd, False, True)
+    def swap(ps, even, odd, mats, tokens, first, first_tokens=()):
+        need("t", *first_tokens)
+        for n, (lhs, rhs) in enumerate(first):
+            mm(ps[:, 0:16], lhs, rhs, n == 0, False)
+        need("t", *tokens)
+        for cols, m in ((slice(1, 16, 2), 256), (slice(0, 16, 2), 0)):
+            mm(ps[:, cols], mats[:, m:m + 128], even, False, False)
+            call = mm(ps[:, cols], mats[:, m + 128:m + 256], odd, False, m == 0)
         return done("t", call)
 
-    second = (T.c16[:], T.ones[:, 0:8])
-    plus_k = (T.c16h[:], T.kh[:, 0:8])
-    place = [0]
-
-    def order_bytes(n):
-        p = place[0]
-        place[0] = p + n
-        return act(T.bt[:, 1 + p:1 + p + n], T.win[:].indirect(T.order[:, p // 16:(p + n) // 16]), COPY)
+    second = [(T.c16[:], T.odd1[:])]
+    plus_k = (T.c16h[:], T.kh[:])
+    plus_4096 = (T.c16[:], T.two[:])
 
     need("v", ("dx", 32))
     n2 = ts(T.sl0[:], T.x0[:], 2047, None, A.bitwise_and)
-    vxs = ts(T.xf[:, 0:16], T.x0[:], float(K), None, A.add)
+    n1 = ts(T.y0[:], T.x0[:], 11, None, A.arith_shift_right)
     need("v", n2)
     n3 = v(g.vector.tensor_copy(T.sh0[:], T.sl0[:]))
-    need("t", vc16, vsw)
-    tx = swap(T.psb1, T.sh0[:, 0:16:2], T.sh0[:, 1:16:2], T.swh, (n3,), second)
-    need("v", k3)
-    for r in range(2):
-        for b in range(2):
-            o = 64 - 16 * r + 64 * b
-            vtri = ts(T.tri[:, 128 * r + 64 * b:128 * r + 64 * b + 64], T.rowkey[:, o:o + 64], T.colk[:, r:r + 1], T.flags[:, 2 + b:3 + b], A.is_gt, A.mult)
-    need("a", k3, c3)
-    for r in range(2, 4):
-        o = 64 - 16 * r
-        asg = act(T.sgn[:, 128 * r - 256:128 * r - 128], T.rowkey[:, o:o + 128], AF.Sign, bias=T.colk[:, 4 + r:5 + r])
-    for b in range(2):
-        act(T.allm[:, 64 * b:64 * b + 64], T.rowkey[:, 0:64], AF.Identity, bias=T.flags[:, 2 + b:3 + b], scale=0.0)
-    need("a", asg)
-    for r in range(2, 4):
-        for b in range(2):
-            atri = act(T.tri[:, 128 * r + 64 * b:128 * r + 64 * b + 64], T.sgn[:, 128 * r - 256 + 64 * b:128 * r - 192 + 64 * b], AF.Relu, scale=T.flags[:, 2 + b:3 + b])
+    tx = swap(T.psb1, T.sh0[:, 0:16:2], T.sh0[:, 1:16:2], T.swh, (n3,), second, (vc16, vodd, vsw))
+    vxs = ts(T.xf[:, 0:16], T.x0[:], float(K - 4096), None, A.add)
+    need("v", to)
+    vorder = v(g.vector.tensor_copy(T.order[:], T.pso[:, 0:128]))
+    need("v", cp)
+    pk = T.colp[:, 0:1]
+    ts(T.part[:, 1:2], pk, 1.0, None, A.is_equal)
+    pb = ts(T.part[:, 2:3], pk, 8.0, None, A.is_equal)
+    pd = ts(T.part[:, 0:1], pk, 0.0, float(2.0 ** -11 + 2.0 ** -34), A.is_equal, A.mult)
+    ts(T.part[:, 3:4], pk, 0.0, BIG - 0.5, A.is_equal, A.mult)
+    pc = ts(T.part[:, 4:5], pk, 4.0, -(BIG + 2047.0), A.is_equal, A.mult)
+    need("v", pb)
+    pd = tt(T.part[:, 5:6], T.part[:, 1:2], T.part[:, 2:3], A.add)
+    need("v", tx)
+    vl = v(g.vector.tensor_copy(T.lst[:, 0:16], T.psb1[:, 0:16]))
+    need("v", pc, pd)
+    tt(T.sc[:, 1:2], T.part[:, 3:4], T.part[:, 4:5], A.add)
+    vsc = tt(T.sc[:, 0:1], T.part[:, 0:1], T.part[:, 5:6], A.add)
+    need("v", n1, kd)
+    vyn = ts(T.d0[:, 2:64:4], T.y0[:], -1.0, -2048.0, A.mult, A.add)
+    vlift = ts(T.lift[:], T.dm[:], 0.0, 255.0 * 4096.0, A.is_equal, A.mult)
     need("v", vsw)
     v(g.vector.tensor_copy(T.swb[:], T.swh[:]))
     need("v", v1, vc16)
     v(g.vector.tensor_copy(T.c16h[:], T.c16[:]))
+    v(g.vector.memset(T.two[:], 2.0))
     vswb = ts(T.kh[:], T.ones[:], 2047.0, None, A.mult)
-    need("v", tx)
-    vl = v(g.vector.tensor_copy(T.lst[:, 0:16], T.psb1[:, 0:16]))
+    need("a", k3, c3)
+    for r in range(4):
+        o = 64 - 16 * r
+        asg = act(T.sgn[:, 128 * r:128 * r + 128], T.rowkey[:, o:o + 128], AF.Sign, bias=T.colk[:, 4 + r:5 + r])
+    for b in range(2):
+        act(T.allm[:, 64 * b:64 * b + 64], T.rowkey[:, 0:64], AF.Identity, bias=T.flags[:, 2 + b:3 + b], scale=0.0)
+    need("a", asg)
+    for r in range(4):
+        for b in range(2):
+            atri = act(T.tri[:, 128 * r + 64 * b:128 * r + 64 * b + 64], T.sgn[:, 128 * r + 64 * b:128 * r + 64 * b + 64], AF.Relu, scale=T.flags[:, 2 + b:3 + b])
 
-    need("a", ("dpool", 128), ("dwin", 128), vorder)
-    have = order_bytes(1024)
-    before = (0, 704, 704, 704, 704)
-    after = (320, 320, 320, 320, 0)
+    need("a", vorder, *loaded)
+
+    def quarter(tile, c0, n):
+        return act(tile, T.win[:].indirect(T.order[:, c0:c0 + n // 16]), COPY)
+
+    def hand_round(tile, token, at, n, sem):
+        need("y", token)
+        for i in range(4):
+            for j in range(4):
+                g.sync.dma_start(T.bt[16 * j + 2:16 * j + 67:64, at + n * i:at + n * i + n], tile[16 * i + 2:16 * i + 67:64, :]).then_inc(T.sem[sem], 16)
+        return (sem, 256)
+
+    aqa = quarter(T.qa[:], 64, 256)
+    have0 = act(T.bt[:, Z:Z + 1024], T.win[:].indirect(T.order[:, 0:64]), COPY)
+    have1 = hand_round(T.qa, aqa, Z + 1024, 256, "dqa")
+
     for s in range(S):
         c = slice(16 * s, 16 * s + 16)
         ev = slice(16 * s, 16 * s + 16, 2)
         od = slice(16 * s + 1, 16 * s + 16, 2)
         nx = slice(16 * s + 16, 16 * s + 32)
         w0 = 256 * s
+        more = s < S - 1
         psa, psb, psc = T["psa%d" % (s % 2)], T["psb%d" % (s % 2)], T["psc%d" % (s % 2)]
 
         def cut(n):
             m = 16 * s + n
             return slice(16 * s, m), slice(m, 16 * s + 16), slice(w0, 16 * m), slice(16 * m, w0 + 256)
 
-        if s:
-            need("t", atri)
+        need("t", atri)
         for q in range(s):
             mm(psc[:, 0:1], T.allm[:], T.cs[:, 16 * q + 15:16 * q + 16], q == 0, False)
-        need("v", vl, ("dpool", 128), ("dwin", 128))
+        need("v", vl, vsc, *loaded)
         tables = T.win[:, 0:4096]
-        clo, chi, lo, hi = cut(6 if s else 16)
-        vr = v(g.vector.tensor_copy(T.ra[:, lo], tables.indirect(T.lst[:, clo])))
+        clo, chi, lo, hi = cut(MODEL if s else 16)
+        vr = ts(T.ra[:, lo], tables.indirect(T.lst[:, clo]), T.sc[:, 0:1], T.sc[:, 1:2], A.mult, A.add)
         if s:
-            need("a", vl)
-            ar = act(T.ra[:, hi], tables.indirect(T.lst[:, chi]), COPY)
-            have = order_bytes(before[s])
+            need("a", vl, vsc)
+            ar = act(T.ra[:, hi], tables.indirect(T.lst[:, chi]), AF.Identity, bias=T.sc[:, 1:2], scale=T.sc[:, 0:1])
+            if s == 1:
+                have2 = hand_round(T.qb, quarter(T.qb[:, 128:768], 88, 640), Z + 2048, 768, "dqb")
             need("v", tby)
             vxs = tt(T.xf[:, c], T["psa%d" % ((s - 1) % 2)][:, 0:16], T.xwi[:, 16 * s - 16:16 * s], A.add)
         xs = T.xf[:, c]
         need("v", vr)
         vt = v(g.vector.transpose(T.ta[:, lo], T.ra[:, lo]))
-        e = T.ta[:, w0:w0 + 256:16]
-        need("v", vxs)
-        ts(T.yh[:, c], xs, 1.0 / 2048, 0.500244140625, A.mult, A.add)
         if s:
             need("v", ar)
             vt = v(g.vector.transpose(T.ta[:, hi], T.ra[:, hi]))
-        need("v", vt)
-        vg = ts(T.gg[:, c], e, 1.0 / 2048, -2047.499755859375, A.mult, A.add)
-        vq = tt(T.q2[:, c], xs, e, A.subtract)
-        need("v", vg)
-        vt2 = tt(T.t2[:, c], T.gg[:, c], T.yh[:, c], A.mult)
-        need("v", vq)
-        vrr = ts(T.rr[:, c], T.q2[:, c], -1.0, 4096.0, A.mult, A.add)
-        need("v", vt2, vrr)
-        vw = tt(T.wr[:, c], T.t2[:, c], T.rr[:, c], A.is_lt)
-        vxn = tt(T.xn[:, c], T.t2[:, c], T.q2[:, c], A.add)
+        need("v", vt, vyn)
+        vst = v(g.vector.tensor_tensor_scan(T.st[:, 64 * s:64 * s + 64], T.d0[:, 64 * s:64 * s + 64], T.ta[:, w0:w0 + 256:4], 0.0, A.mult, A.add))
+        st = T.st[:, 64 * s + 2:64 * s + 64:4]
+        need("v", vst, vxs)
+        vw = tt(T.wr[:, c], st, xs, A.is_gt)
+        vxn = tt(T.xn[:, c], xs, st, A.subtract)
         need("v", vw)
         vcs = v(g.vector.tensor_tensor_scan(T.cs[:, c], T.ones[:], T.wr[:, c], 0.0, A.mult, A.add))
-        need("t", vcs, vtri)
+        need("t", vcs)
         r = s % 4
         tb = done("t", mm(psc[:, 0:1], T.tri[:, 128 * r:128 * r + 128], T.cs[:, 16 * s + 15:16 * s + 16], s == 0, True))
         vm = ts(T.mm[:, c], T.wr[:, c], 255.0, 1.0, A.mult, A.add)
-        vu = ts(T.uu[:, c], T.wr[:, c], 8192.0, -8192.0, A.mult, A.add)
+        vu = ts(T.uu[:, c], T.wr[:, c], 8192.0, float(Z - 1 - 8192), A.mult, A.add)
+        if more:
+            vmy = ts(T.my[:, c], T.wr[:, c], -510.0, -2050.0, A.mult, A.add)
         need("v", vm, vxn)
         vxw = tt(T.xwi[:, c], T.mm[:, c], T.xn[:, c], A.mult)
         need("v", vu, vcs)
         vv = tt(T.vv[:, c], T.uu[:, c], T.cs[:, c], A.add)
-        if s < S - 1:
+        if more:
             need("v", vxw)
             vsl = ts(T.sl[:, c], T.xwi[:, c], 2047, None, A.bitwise_and)
         need("v", vv, tb)
         vi = ts(T.idx[:, c], T.vv[:, c], psc[:, 0:1], None, A.add)
-        if s < S - 1:
+        if more:
             need("v", vsl)
             vsh = v(g.vector.tensor_copy(T.sh[:, c], T.sl[:, c]))
             tsl = swap(psb, T.sh[:, ev], T.sh[:, od], T.swh, (vsh,), second)
-        table = T.bt[:, 0:1025 + 1024 * s]
-        clo, chi, lo, hi = cut(8)
-        need("v", vi, have)
+        need("a", vt)
+        sy = T.res1[:, c] if more else T.res3[:]
+        asy = act(sy, T.ta[:, w0 + 1:w0 + 256:16], COPY)
+        have = (have0,) if s == 0 else (have0, have1) if s == 1 else (have0, have1, have2)
+        table = T.bt[:, 0:Z + 1024 + 1024 * s]
+        clo, chi, lo, hi = cut(BYTE)
+        need("v", vi, *have)
         vrb = v(g.vector.tensor_copy(T.rb[:, lo], table.indirect(T.idx[:, clo])))
-        need("a", vi, have)
+        if more:
+            vyy = ts(T.yy[:, c], T.xwi[:, c], 11, None, A.arith_shift_right)
+        need("a", vi, *have)
         arb = act(T.rb[:, hi], table.indirect(T.idx[:, chi]), COPY)
+        if s == 0:
+            quarter(T.qb[:, 0:128], 80, 128)
         need("v", vrb)
         v(g.vector.transpose(T.tb[:, lo], T.rb[:, lo]))
         need("v", arb)
         vtb = v(g.vector.transpose(T.tb[:, hi], T.rb[:, hi]))
         byte = T.tb[:, w0 + 2:w0 + 256:16]
-        need("t", vswb)
-        const = plus_k if s < S - 1 else None
-        tby = swap(psa, T.tb[:, w0 + 2:w0 + 256:32], T.tb[:, w0 + 18:w0 + 256:32], T.swb, (vtb,), const, const)
-        need("a", vt)
-        sy = T.res1[:, c] if s < S - 1 else T.res2[:, 16:32]
-        asy = act(sy, T.ta[:, w0 + 1:w0 + 256:16], COPY)
-        if after[s]:
-            have = order_bytes(after[s])
+        const = plus_k if more else plus_4096
+        tby = swap(psa, T.tb[:, w0 + 2:w0 + 256:32], T.tb[:, w0 + 18:w0 + 256:32], T.swb, (vtb,),
+                   [const, (T.lift[:], T.wr[:, c])], (vw, vlift, vswb))
         if s == S - 2:
             need("g", asy)
             same(T.res1[:], T.back1, "r1")
             need("y", asy)
             g.sync.dma_start(T.back1[rank], T.res1[:]).then_inc(T.sem.dback1, 16)
-        if s < S - 1:
+        if more:
+            need("v", vmy, vyy)
+            vyn = tt(T.d0[:, 64 * s + 66:64 * s + 128:4], T.my[:, c], T.yy[:, c], A.subtract)
             need("v", vtb, tsl)
             vsf = tt(T.slf[:, nx], psb[:, 0:16], byte, A.add)
             need("v", vsf)
             vl = v(g.vector.tensor_copy(T.lst[:, nx], T.slf[:, nx]))
         else:
             need("v", tby)
-            vlast = tt(T.res2[:, 0:16], psa[:, 0:16], T.xwi[:, c], A.add)
+            vlast = tt(T.res2[:], psa[:, 0:16], T.xwi[:, c], A.add)
 
-    need("g", vlast, asy)
+    mine = [slice(64 * sg + 16 * rank, 64 * sg + 16 * rank + 16) for sg in range(2)]
+    need("g", asy)
+    same(T.res3[:], T.back3, "r3")
+    need("g", vlast)
     same(T.res2[:], T.back2, "r2")
     need("y", ("r1", 24), ("dback1", 16))
-    mine = [slice(64 * sg + 16 * rank, 64 * sg + 16 * rank + 16) for sg in range(2)]
-    need("a", vlast, asy)
-    g.scalar.dma_start(T.back2[rank], T.res2[:]).then_inc(T.sem.dback2, 16)
     for s in range(S - 1):
         for sg in range(2):
             g.sync.dma_start(T.syms[sg:8:2, L * s:L * s + L], T.back1[:, mine[sg], 16 * s:16 * s + 16]).then_inc(T.sem.dout, 16)
-    need("y", ("r2", 24), ("dback2", 16))
+    need("a", asy)
+    g.scalar.dma_start(T.back3[rank], T.res3[:]).then_inc(T.sem.dback3, 16)
+    need("y", vlast)
+    g.sync.dma_start(T.back2[rank], T.res2[:]).then_inc(T.sem.dback2, 16)
+    need("a", ("r3", 24), ("dback3", 16))
     for sg in range(2):
-        g.sync.dma_start(T.last[sg:8:2, :], T.back2[:, mine[sg], 0:16]).then_inc(T.sem.dout, 16)
-    need("a", ("r2", 24), ("dback2", 16))
-    for sg in range(2):
-        g.scalar.dma_start(T.syms[sg:8:2, L * (S - 1):L * S], T.back2[:, mine[sg], 16:32]).then_inc(T.sem.dout2, 16)
-    need("y", ("dout", 160))
-    need("a", ("dout2", 32))
-    need("g", ("loc", 28), ("v", count["v"]), ("a", count["a"]), ("t", count["t"]), ("k", count["k"]))
+        g.scalar.dma_start(T.syms[sg:8:2, L * (S - 1):L * S], T.back3[:, mine[sg], :]).then_inc(T.sem.dout2, 16)
+    for sg, q in enumerate("ya"):
+        need(q, ("r2", 24), ("dback2", 16))
+        queues[q].dma_start(T.last[sg:8:2, :], T.back2[:, mine[sg], :]).then_inc(T.sem[("dout", "dout2")[sg]], 16)
+    need("y", ("dout", 144))
+    need("a", ("dout2", 48))
+    need("g", ("loc", 36), ("v", count["v"]), ("a", count["a"]), ("t", count["t"]), ("k", count["k"]))

import numpy as np
from concourse.bass import DstId, RemoteDMATransfer
from concourse.mybir import dt, AluOpType, ActivationFunctionType

SCRATCH = {
    "stgm": ("dram", [4, 128, 64], "int32"), "landm": ("dram", [4, 128, 64], "int32"),
    "stgs": ("dram", [4, 128, 32], "int32"), "lands": ("dram", [4, 128, 32], "int32"),
    "back1": ("dram", [4, 128, 64], "float32"), "back2": ("dram", [4, 128, 16], "float32"), "back3": ("dram", [4, 128, 16], "float32"),
    "win": ("sbuf", [128, 5120], "int32"), "bt": ("sbuf", [128, 5136], "bfloat16"),
    "qa": ("sbuf", [128, 256], "bfloat16"), "qb": ("sbuf", [128, 768], "bfloat16"),
    "pl": ("sbuf", [128, 8, 16], "int32"), "pa": ("sbuf", [128, 8, 16], "int32"), "pb": ("sbuf", [128, 8, 16], "int32"),
    "ha": ("sbuf", [128, 8, 48], "float16"), "hb": ("sbuf", [128, 8, 48], "float16"), "zz": ("sbuf", [128, 8, 16], "bfloat16"),
    "sraw": ("sbuf", [128, 4, 32], "float32"), "sela": ("sbuf", [128, 4, 32], "float16"), "selb": ("sbuf", [128, 4, 32], "float16"),
    "order": ("sbuf", [128, 128], "uint16"), "pso": ("psum", [128, 512], "float32"),
    "dm": ("sbuf", [128, 128], "float32"), "rowkey": ("sbuf", [128, 256], "float32"),
    "coli": ("sbuf", [128, 8], "int32"), "colj": ("sbuf", [128, 8], "int32"), "colk": ("sbuf", [128, 8], "float32"),
    "colp": ("sbuf", [128, 8], "int32"), "part": ("sbuf", [128, 8], "float32"), "sc": ("sbuf", [128, 4], "float32"),
    "flags": ("sbuf", [128, 4], "float32"), "swh": ("sbuf", [128, 512], "float16"), "swb": ("sbuf", [128, 512], "bfloat16"),
    "c16": ("sbuf", [128, 128], "bfloat16"), "c16h": ("sbuf", [128, 128], "float16"), "kh": ("sbuf", [128, 16], "float16"),
    "tri": ("sbuf", [128, 512], "bfloat16"), "allm": ("sbuf", [128, 128], "bfloat16"), "ones": ("sbuf", [128, 16], "bfloat16"),
    "two": ("sbuf", [128, 16], "bfloat16"), "odd1": ("sbuf", [128, 16], "bfloat16"), "lift": ("sbuf", [128, 128], "bfloat16"),
    "sgn": ("sbuf", [128, 512], "bfloat16"),
    "x0": ("sbuf", [128, 16], "int32"), "sl0": ("sbuf", [128, 16], "int32"), "y0": ("sbuf", [128, 16], "int32"),
    "sh0": ("sbuf", [128, 16], "float16"),
    "xf": ("sbuf", [128, 80], "float32"), "slf": ("sbuf", [128, 80], "float32"),
    "lst": ("sbuf", [128, 80], "uint16"), "ra": ("sbuf", [128, 1280], "float32"), "ta": ("sbuf", [128, 1280], "float32"),
    "yy": ("sbuf", [128, 80], "int32"), "my": ("sbuf", [128, 80], "float32"),
    "d0": ("sbuf", [128, 320], "float32"), "st": ("sbuf", [128, 320], "float32"),
    "xn": ("sbuf", [128, 80], "float32"), "wr": ("sbuf", [128, 80], "bfloat16"),
    "cs": ("sbuf", [128, 80], "bfloat16"), "mm": ("sbuf", [128, 80], "float32"), "xwi": ("sbuf", [128, 80], "int32"),
    "sl": ("sbuf", [128, 80], "int32"), "sh": ("sbuf", [128, 80], "float16"),
    "uu": ("sbuf", [128, 80], "float32"), "vv": ("sbuf", [128, 80], "float32"), "idx": ("sbuf", [128, 80], "uint16"),
    "rb": ("sbuf", [128, 1280], "bfloat16"), "tb": ("sbuf", [128, 1280], "bfloat16"),
    "res1": ("sbuf", [128, 64], "float32"), "res2": ("sbuf", [128, 16], "float32"), "res3": ("sbuf", [128, 16], "float32"),
    "psa0": ("psum", [128, 512], "float32"), "psa1": ("psum", [128, 512], "float32"),
    "psb0": ("psum", [128, 512], "float32"), "psb1": ("psum", [128, 512], "float32"),
    "psc0": ("psum", [128, 512], "float32"), "psc1": ("psum", [128, 512], "float32"),
}
SEMAPHORES = ["v", "a", "t", "k", "dstm", "dsts", "downm", "downs", "dpl", "dfill", "dwin", "dx", "dpool", "dqa", "dqb",
              "rs", "rm", "r1", "r2", "r3", "loc", "dback1", "dback2", "dback3", "dout", "dout2"]


def rank_program(g, core, T, topo):
    rank = T.rank_of(core)
    if rank is None:
        return
    A = AluOpType
    AF = ActivationFunctionType
    COPY = AF.Copy
    S, L = 5, 256
    others = [c for c in T.cores if c != core]
    K = 2047 * 2048
    FILL = 3520
    Z = 16
    MODEL, BYTE = 6, 8
    BIG = 2.0 ** 23

    queues = {"g": g, "v": g.vector, "a": g.scalar, "t": g.tensor, "y": g.sync}
    count = {"v": 0, "a": 0, "t": 0, "k": 0}
    seen = {}

    def need(q, *tokens):
        for name, n in tokens:
            if n > seen.get((q, name), 0):
                queues[q].wait_ge(T.sem[name], n)
                seen[(q, name)] = n

    def done(name, call):
        call.then_inc(T.sem[name], 1)
        count[name] += 1
        return (name, count[name])

    def v(call):
        return done("v", call)

    def ts(out, in0, s1, s2, op0, op1=None):
        if op1 is None:
            return v(g.vector.tensor_scalar(out, in0, s1, s2, op0))
        return v(g.vector.tensor_scalar(out, in0, s1, s2, op0, op1))

    def tt(out, a, b, op):
        return v(g.vector.tensor_tensor(out, a, b, op))

    def act(*args, **kw):
        return done("a", g.scalar.activation(*args, **kw))

    def dst(c):
        rid, pid, _ = topo.addr(c)
        return DstId(rid=rid, pnc=pid)

    def bits(engines):
        m = 0
        for e in engines:
            m |= 1 << e
        return m

    def spread(src, land, sem):
        out = []
        for i, c in enumerate(others):
            es = topo.engines(core, c)
            out.append(RemoteDMATransfer(src=src[T.rank_of(c)], dst=land[rank], dst_ids=[dst(c)],
                                         dma_engine_mask=bits(es[2 * i:2 * i + 2]), remote_sem=T.sem[sem]))
        g.remote_dma_fused(out, local_sem=T.sem.loc)

    def same(src, land, sem):
        es = topo.engines(core, others[0])
        g.remote_dma_fused([RemoteDMATransfer(srcs=[src], dsts=[land[rank] for c in others], dst_ids=[dst(c) for c in others],
                                              dma_engine_mask=bits(es), remote_sem=T.sem[sem])], local_sem=T.sem.loc)

    own = slice(2 * rank, 2 * rank + 2)
    g.scalar.dma_start(T.stgs[:, 0:80, :], T.stock[:]).then_inc(T.sem.dsts, 16)
    g.scalar.dma_start(T.stgs[:, 80:96, :], T.states[:]).then_inc(T.sem.dsts, 16)
    g.scalar.dma_start(T.stgs[:, 96:128, :], T.letters[0:2, :]).then_inc(T.sem.dsts, 16)
    g.sync.dma_start(T.stgm[:, 0:64, :], T.models[:]).then_inc(T.sem.dstm, 16)
    g.sync.dma_start(T.stgm[:, 64:128, :], T.letters[:]).then_inc(T.sem.dstm, 16)
    for sg in range(2):
        g.scalar.dma_start(T.pl[0:80, 4 * sg:4 * sg + 4, :], T.places[2 * rank + sg, :]).then_inc(T.sem.dpl, 16)
    g.sync.dma_start(T.landm[rank, 0:64, :], T.models[own, :]).then_inc(T.sem.downm, 16)
    g.sync.dma_start(T.landm[rank, 64:128, :], T.letters[own, :]).then_inc(T.sem.downm, 16)
    g.sync.dma_start(T.lands[rank, 0:80, :], T.stock[own, :]).then_inc(T.sem.downs, 16)
    g.sync.dma_start(T.lands[rank, 80:96, :], T.states[own, :]).then_inc(T.sem.downs, 16)
    fills = range(FILL, 5120, 320)
    for a in fills:
        g.sync.dma_start(T.win[:, a:a + 320], T.places[:]).then_inc(T.sem.dfill, 16)
    filled = ("dfill", 16 * len(fills))

    done("k", g.iota(T.coli[:, 0:4], [[-16, 4]], 64, 1))
    done("k", g.iota(T.coli[:, 4:8], [[0, 4]], 0, 1))
    done("k", g.iota(T.sraw[:, :, 0:16], [[0, 4], [1, 16]], 0, -1, allow_small_or_imprecise_dtypes=True))
    done("k", g.iota(T.sraw[:, :, 16:20], [[4, 4], [1, 4]], 16, -1, allow_small_or_imprecise_dtypes=True))
    k1 = done("k", g.iota(T.sraw[:, :, 20:32], [[12, 4], [1, 12]], 32, -1, allow_small_or_imprecise_dtypes=True))
    need("g", ("dsts", 48))
    spread(T.stgs, T.lands, "rs")
    need("g", ("dstm", 32))
    spread(T.stgm, T.landm, "rm")
    k2 = done("k", g.iota(T.dm[:], [[1, 128]], 0, -1, allow_small_or_imprecise_dtypes=True))
    k3 = done("k", g.iota(T.rowkey[:], [[0, 4], [1, 64]], 0, 0, allow_small_or_imprecise_dtypes=True))
    kd = done("k", g.iota(T.d0[:], [[0, 320]], 1, 0, allow_small_or_imprecise_dtypes=True))
    need("g", kd)
    kd = done("k", g.iota(T.d0[:, 0:320:4], [[0, 80]], 0, 0, allow_small_or_imprecise_dtypes=True))

    mm = g.tensor.matmul

    v(g.vector.memset(T.bt[:, 0:Z], 0.0))
    vseed = v(g.vector.memset(T.bt[:, 1040:1552], 0.0))
    v(g.vector.memset(T.win[:, 0:FILL // 2], 0))
    vz = v(g.vector.memset(T.zz[:], 0.0))
    need("v", ("dpl", 32))
    p1 = ts(T.pa[0:80, :, :], T.pl[0:80, :, :], 3, None, A.bitwise_and)
    p2 = ts(T.pb[0:80, :, :], T.pl[0:80, :, :], 2, None, A.arith_shift_right)
    need("v", vz)
    for h in (T.ha, T.hb):
        v(g.vector.tensor_copy(h[0:80, :, 0:16], T.zz[0:80, :, :]))
        v(g.vector.tensor_copy(h[0:80, :, 32:48], T.zz[0:80, :, :]))
    need("v", k1)
    ts(T.sela[:], T.sraw[:], 0.0, 1280.0, A.is_equal, A.mult)
    ts(T.selb[:], T.sraw[:], 0.0, None, A.is_equal)
    need("v", p2)
    v(g.vector.tensor_copy(T.ha[0:80, :, 16:32], T.pa[0:80, :, :]))
    vh = v(g.vector.tensor_copy(T.hb[0:80, :, 16:32], T.pb[0:80, :, :]))
    need("t", vh)
    for a in range(4):
        for q in range(4):
            o = T.pso[32 * a:32 * a + 32, q:128:4]
            for b in range(2):
                i, w = 2 * (a % 2) + b, slice(16 - 16 * b, 48 - 16 * b)
                mm(o, T.ha[0:80, 4 * (a // 2) + q, w], T.sela[0:80, i, :], b == 0, False)
                call = mm(o, T.hb[0:80, 4 * (a // 2) + q, w], T.selb[0:80, i, :], False, b == 1)
    to = done("t", call)
    vwin = v(g.vector.memset(T.win[:, FILL // 2:FILL], 0))
    ts(T.colj[:, 0:4], T.coli[:, 0:4], 63, None, A.bitwise_and)
    c2 = ts(T.colj[:, 4:8], T.coli[:, 4:8], 16, None, A.bitwise_and)
    cp = ts(T.colp[:, 0:4], T.coli[:, 4:8], 15, None, A.bitwise_and)
    ts(T.flags[:, 2:3], T.coli[:, 4:5], 64.0, None, A.is_lt)
    ts(T.flags[:, 3:4], T.coli[:, 4:5], 64.0, None, A.is_ge)
    need("v", c2)
    v(g.vector.tensor_copy(T.colk[:, 0:4], T.colj[:, 0:4]))
    c3 = ts(T.colk[:, 4:8], T.colj[:, 0:4], -1.0, None, A.mult)
    ts(T.flags[:, 0:1], T.colj[:, 4:5], 0.0, None, A.is_equal)
    cf = ts(T.flags[:, 1:2], T.colj[:, 4:5], 16.0, None, A.is_equal)
    vodd = v(g.vector.memset(T.odd1[:], 0.0))
    v1 = v(g.vector.memset(T.ones[:], 1.0))
    vc16 = v(g.vector.memset(T.c16[:], 16.0))
    need("v", vodd)
    vodd = v(g.vector.memset(T.odd1[:, 1:16:2], 1.0))
    need("v", k2, cf)
    for i, (d, f) in enumerate(((0.0, 0), (16.0, 0), (-16.0, 1), (0.0, 1))):
        vsw = ts(T.swh[:, 128 * i:128 * i + 128], T.dm[:], d, T.flags[:, f:f + 1], A.is_equal, A.mult)

    need("a", vseed)
    for a, n in ((1552, 512), (2064, 1024), (3088, 2048)):
        need("a", ("a", count["a"]))
        act(T.bt[:, a:a + n], T.bt[:, a - n:a], COPY)

    def load_pool(queue, i):
        sg = i // 4
        queue.dma_start(T.win[16 * i + 2:16 * i + 3, :], T.lands[:, 40 * sg:40 * sg + 40, :]).then_inc(T.sem.dpool, 16)

    def load_table(queue, kind, at, sg):
        for ga in range(2):
            p = 64 * sg + 16 * ga + at
            queue.dma_start(T.win[p:p + 33:32, 0:4096], T.landm[:, 64 * kind + 32 * sg:64 * kind + 32 * sg + 32, :]).then_inc(T.sem.dwin, 16)

    need("y", ("downs", 32), ("rs", 6))
    for sg in range(2):
        g.sync.dma_start(T.x0[64 * sg:64 * sg + 64, :], T.lands[:, 80 + 8 * sg:88 + 8 * sg, :]).then_inc(T.sem.dx, 16)
    need("y", vwin, filled)
    need("a", ("downs", 32), ("rs", 6), vwin, filled)
    for i in range(4):
        load_pool(g.scalar, i)
        load_pool(g.sync, 4 + i)
    need("y", ("downm", 32), ("rm", 6))
    need("a", ("downm", 32), ("rm", 6))
    for kind, at in ((0, 0), (0, 8), (1, 1)):
        load_table(g.sync, kind, at, 0)
        load_table(g.scalar, kind, at, 1)
    loaded = (("dpool", 128), ("dwin", 192))

    def swap(ps, even, odd, mats, tokens, first, first_tokens=()):
        need("t", *first_tokens)
        for n, (lhs, rhs) in enumerate(first):
            mm(ps[:, 0:16], lhs, rhs, n == 0, False)
        need("t", *tokens)
        for cols, m in ((slice(1, 16, 2), 256), (slice(0, 16, 2), 0)):
            mm(ps[:, cols], mats[:, m:m + 128], even, False, False)
            call = mm(ps[:, cols], mats[:, m + 128:m + 256], odd, False, m == 0)
        return done("t", call)

    second = [(T.c16[:], T.odd1[:])]
    plus_k = (T.c16h[:], T.kh[:])
    plus_4096 = (T.c16[:], T.two[:])

    need("v", ("dx", 32))
    n2 = ts(T.sl0[:], T.x0[:], 2047, None, A.bitwise_and)
    n1 = ts(T.y0[:], T.x0[:], 11, None, A.arith_shift_right)
    need("v", n2)
    n3 = v(g.vector.tensor_copy(T.sh0[:], T.sl0[:]))
    tx = swap(T.psb1, T.sh0[:, 0:16:2], T.sh0[:, 1:16:2], T.swh, (n3,), second, (vc16, vodd, vsw))
    vxs = ts(T.xf[:, 0:16], T.x0[:], float(K - 4096), None, A.add)
    need("v", to)
    vorder = v(g.vector.tensor_copy(T.order[:], T.pso[:, 0:128]))
    need("v", cp)
    pk = T.colp[:, 0:1]
    ts(T.part[:, 1:2], pk, 1.0, None, A.is_equal)
    pb = ts(T.part[:, 2:3], pk, 8.0, None, A.is_equal)
    pd = ts(T.part[:, 0:1], pk, 0.0, float(2.0 ** -11 + 2.0 ** -34), A.is_equal, A.mult)
    ts(T.part[:, 3:4], pk, 0.0, BIG - 0.5, A.is_equal, A.mult)
    pc = ts(T.part[:, 4:5], pk, 4.0, -(BIG + 2047.0), A.is_equal, A.mult)
    need("v", pb)
    pd = tt(T.part[:, 5:6], T.part[:, 1:2], T.part[:, 2:3], A.add)
    need("v", tx)
    vl = v(g.vector.tensor_copy(T.lst[:, 0:16], T.psb1[:, 0:16]))
    need("v", pc, pd)
    tt(T.sc[:, 1:2], T.part[:, 3:4], T.part[:, 4:5], A.add)
    vsc = tt(T.sc[:, 0:1], T.part[:, 0:1], T.part[:, 5:6], A.add)
    need("v", n1, kd)
    vyn = ts(T.d0[:, 2:64:4], T.y0[:], -1.0, -2048.0, A.mult, A.add)
    vlift = ts(T.lift[:], T.dm[:], 0.0, 255.0 * 4096.0, A.is_equal, A.mult)
    need("v", vsw)
    v(g.vector.tensor_copy(T.swb[:], T.swh[:]))
    need("v", v1, vc16)
    v(g.vector.tensor_copy(T.c16h[:], T.c16[:]))
    v(g.vector.memset(T.two[:], 2.0))
    vswb = ts(T.kh[:], T.ones[:], 2047.0, None, A.mult)
    need("a", k3, c3)
    for r in range(4):
        o = 64 - 16 * r
        asg = act(T.sgn[:, 128 * r:128 * r + 128], T.rowkey[:, o:o + 128], AF.Sign, bias=T.colk[:, 4 + r:5 + r])
    for b in range(2):
        act(T.allm[:, 64 * b:64 * b + 64], T.rowkey[:, 0:64], AF.Identity, bias=T.flags[:, 2 + b:3 + b], scale=0.0)
    need("a", asg)
    for r in range(4):
        for b in range(2):
            atri = act(T.tri[:, 128 * r + 64 * b:128 * r + 64 * b + 64], T.sgn[:, 128 * r + 64 * b:128 * r + 64 * b + 64], AF.Relu, scale=T.flags[:, 2 + b:3 + b])

    need("a", vorder, *loaded)

    def quarter(tile, c0, n):
        return act(tile, T.win[:].indirect(T.order[:, c0:c0 + n // 16]), COPY)

    def hand_round(tile, token, at, n, sem):
        need("y", token)
        for i in range(4):
            for j in range(4):
                g.sync.dma_start(T.bt[16 * j + 2:16 * j + 67:64, at + n * i:at + n * i + n], tile[16 * i + 2:16 * i + 67:64, :]).then_inc(T.sem[sem], 16)
        return (sem, 256)

    aqa = quarter(T.qa[:], 64, 256)
    have0 = act(T.bt[:, Z:Z + 1024], T.win[:].indirect(T.order[:, 0:64]), COPY)
    have1 = hand_round(T.qa, aqa, Z + 1024, 256, "dqa")

    for s in range(S):
        c = slice(16 * s, 16 * s + 16)
        ev = slice(16 * s, 16 * s + 16, 2)
        od = slice(16 * s + 1, 16 * s + 16, 2)
        nx = slice(16 * s + 16, 16 * s + 32)
        w0 = 256 * s
        more = s < S - 1
        psa, psb, psc = T["psa%d" % (s % 2)], T["psb%d" % (s % 2)], T["psc%d" % (s % 2)]

        def cut(n):
            m = 16 * s + n
            return slice(16 * s, m), slice(m, 16 * s + 16), slice(w0, 16 * m), slice(16 * m, w0 + 256)

        need("t", atri)
        for q in range(s):
            mm(psc[:, 0:1], T.allm[:], T.cs[:, 16 * q + 15:16 * q + 16], q == 0, False)
        need("v", vl, vsc, *loaded)
        tables = T.win[:, 0:4096]
        clo, chi, lo, hi = cut(MODEL if s else 16)
        vr = ts(T.ra[:, lo], tables.indirect(T.lst[:, clo]), T.sc[:, 0:1], T.sc[:, 1:2], A.mult, A.add)
        if s:
            need("a", vl, vsc)
            ar = act(T.ra[:, hi], tables.indirect(T.lst[:, chi]), AF.Identity, bias=T.sc[:, 1:2], scale=T.sc[:, 0:1])
            if s == 1:
                have2 = hand_round(T.qb, quarter(T.qb[:, 128:768], 88, 640), Z + 2048, 768, "dqb")
            need("v", tby)
            vxs = tt(T.xf[:, c], T["psa%d" % ((s - 1) % 2)][:, 0:16], T.xwi[:, 16 * s - 16:16 * s], A.add)
        xs = T.xf[:, c]
        need("v", vr)
        vt = v(g.vector.transpose(T.ta[:, lo], T.ra[:, lo]))
        if s:
            need("v", ar)
            vt = v(g.vector.transpose(T.ta[:, hi], T.ra[:, hi]))
        need("v", vt, vyn)
        vst = v(g.vector.tensor_tensor_scan(T.st[:, 64 * s:64 * s + 64], T.d0[:, 64 * s:64 * s + 64], T.ta[:, w0:w0 + 256:4], 0.0, A.mult, A.add))
        st = T.st[:, 64 * s + 2:64 * s + 64:4]
        need("v", vst, vxs)
        vw = tt(T.wr[:, c], st, xs, A.is_gt)
        vxn = tt(T.xn[:, c], xs, st, A.subtract)
        need("v", vw)
        vcs = v(g.vector.tensor_tensor_scan(T.cs[:, c], T.ones[:], T.wr[:, c], 0.0, A.mult, A.add))
        need("t", vcs)
        r = s % 4
        tb = done("t", mm(psc[:, 0:1], T.tri[:, 128 * r:128 * r + 128], T.cs[:, 16 * s + 15:16 * s + 16], s == 0, True))
        vm = ts(T.mm[:, c], T.wr[:, c], 255.0, 1.0, A.mult, A.add)
        vu = ts(T.uu[:, c], T.wr[:, c], 8192.0, float(Z - 1 - 8192), A.mult, A.add)
        if more:
            vmy = ts(T.my[:, c], T.wr[:, c], -510.0, -2050.0, A.mult, A.add)
        need("v", vm, vxn)
        vxw = tt(T.xwi[:, c], T.mm[:, c], T.xn[:, c], A.mult)
        need("v", vu, vcs)
        vv = tt(T.vv[:, c], T.uu[:, c], T.cs[:, c], A.add)
        if more:
            need("v", vxw)
            vsl = ts(T.sl[:, c], T.xwi[:, c], 2047, None, A.bitwise_and)
        need("v", vv, tb)
        vi = ts(T.idx[:, c], T.vv[:, c], psc[:, 0:1], None, A.add)
        if more:
            need("v", vsl)
            vsh = v(g.vector.tensor_copy(T.sh[:, c], T.sl[:, c]))
            tsl = swap(psb, T.sh[:, ev], T.sh[:, od], T.swh, (vsh,), second)
        need("a", vt)
        sy = T.res1[:, c] if more else T.res3[:]
        asy = act(sy, T.ta[:, w0 + 1:w0 + 256:16], COPY)
        have = (have0,) if s == 0 else (have0, have1) if s == 1 else (have0, have1, have2)
        table = T.bt[:, 0:Z + 1024 + 1024 * s]
        clo, chi, lo, hi = cut(BYTE)
        need("v", vi, *have)
        vrb = v(g.vector.tensor_copy(T.rb[:, lo], table.indirect(T.idx[:, clo])))
        if more:
            vyy = ts(T.yy[:, c], T.xwi[:, c], 11, None, A.arith_shift_right)
        need("a", vi, *have)
        arb = act(T.rb[:, hi], table.indirect(T.idx[:, chi]), COPY)
        if s == 0:
            quarter(T.qb[:, 0:128], 80, 128)
        need("v", vrb)
        v(g.vector.transpose(T.tb[:, lo], T.rb[:, lo]))
        need("v", arb)
        vtb = v(g.vector.transpose(T.tb[:, hi], T.rb[:, hi]))
        byte = T.tb[:, w0 + 2:w0 + 256:16]
        const = plus_k if more else plus_4096
        tby = swap(psa, T.tb[:, w0 + 2:w0 + 256:32], T.tb[:, w0 + 18:w0 + 256:32], T.swb, (vtb,),
                   [const, (T.lift[:], T.wr[:, c])], (vw, vlift, vswb))
        if s == S - 2:
            need("g", asy)
            same(T.res1[:], T.back1, "r1")
            need("y", asy)
            g.sync.dma_start(T.back1[rank], T.res1[:]).then_inc(T.sem.dback1, 16)
        if more:
            need("v", vmy, vyy)
            vyn = tt(T.d0[:, 64 * s + 66:64 * s + 128:4], T.my[:, c], T.yy[:, c], A.subtract)
            need("v", vtb, tsl)
            vsf = tt(T.slf[:, nx], psb[:, 0:16], byte, A.add)
            need("v", vsf)
            vl = v(g.vector.tensor_copy(T.lst[:, nx], T.slf[:, nx]))
        else:
            need("v", tby)
            vlast = tt(T.res2[:], psa[:, 0:16], T.xwi[:, c], A.add)

    mine = [slice(64 * sg + 16 * rank, 64 * sg + 16 * rank + 16) for sg in range(2)]
    need("g", asy)
    same(T.res3[:], T.back3, "r3")
    need("g", vlast)
    same(T.res2[:], T.back2, "r2")
    need("y", ("r1", 24), ("dback1", 16))
    for s in range(S - 1):
        for sg in range(2):
            g.sync.dma_start(T.syms[sg:8:2, L * s:L * s + L], T.back1[:, mine[sg], 16 * s:16 * s + 16]).then_inc(T.sem.dout, 16)
    need("a", asy)
    g.scalar.dma_start(T.back3[rank], T.res3[:]).then_inc(T.sem.dback3, 16)
    need("y", vlast)
    g.sync.dma_start(T.back2[rank], T.res2[:]).then_inc(T.sem.dback2, 16)
    need("a", ("r3", 24), ("dback3", 16))
    for sg in range(2):
        g.scalar.dma_start(T.syms[sg:8:2, L * (S - 1):L * S], T.back3[:, mine[sg], :]).then_inc(T.sem.dout2, 16)
    for sg, q in enumerate("ya"):
        need(q, ("r2", 24), ("dback2", 16))
        queues[q].dma_start(T.last[sg:8:2, :], T.back2[:, mine[sg], :]).then_inc(T.sem[("dout", "dout2")[sg]], 16)
    need("y", ("dout", 144))
    need("a", ("dout2", 48))
    need("g", ("loc", 36), ("v", count["v"]), ("a", count["a"]), ("t", count["t"]), ("k", count["k"]))
